import numpy as np
import ml_dtypes


def mxq(x, axis, fmt="e4m3"):
    dtype, down = {"e4m3": (ml_dtypes.float8_e4m3fn, 7), "e5m2": (ml_dtypes.float8_e5m2, 14)}[fmt]
    v = np.moveaxis(np.asarray(x, np.float32).astype(ml_dtypes.bfloat16).astype(np.float64), axis, -1)
    blocks = v.reshape(v.shape[:-1] + (-1, 32))
    amax = np.abs(blocks).max(-1, keepdims=True)
    byte = np.maximum(np.where(amax > 0, np.frexp(amax)[1] - 1 + 127, 0) - down, 1)
    scale = np.exp2(byte - 127.0)
    codes = (blocks / scale).astype(np.float32).astype(dtype).astype(np.float64)
    return np.moveaxis((codes * scale).reshape(v.shape), -1, axis)


WIDE = False


def mx_kscale(k):
    if not WIDE:
        return np.ones(k)
    levels = np.array([10, -10, 5, -5, 0])
    if k % 512:
        return np.exp2(np.random.permutation(np.resize(levels, k // 32))).repeat(32)
    a = np.empty((k // 512, 16))
    for p in range(k // 512):
        a[p, :8] = np.random.permutation(np.resize(levels, 8))
        for g in range(8):
            far = levels[np.abs(levels - a[p, g]) >= 10]
            a[p, g + 8] = far[np.random.randint(len(far))]
    return np.exp2(a.ravel()).repeat(32)


def f64(x):
    return np.asarray(x).astype(np.float64)


def striped(idx):
    return np.tile(np.asarray(idx).reshape(-1, 16).T, (8, 1)).astype(np.uint16)


def unstriped(offs):
    return offs[:16].T.reshape(-1).astype(np.int64)


E2M1 = np.array([0.0, 0.5, 1.0, 1.5, 2.0, 3.0, 4.0, 6.0, -0.0, -0.5, -1.0, -1.5, -2.0, -3.0, -4.0, -6.0])


def pack_weight(w, fmt):
    k, n = w.shape
    w = f64(np.asarray(w, np.float32).astype(ml_dtypes.bfloat16)).reshape(k // 32, 32, n)
    amax = np.abs(w).max(1)
    if fmt == "e4m3":
        byte = np.frexp(amax)[1] - 1 + 127 - 7
    else:
        mant, ex = np.frexp(amax / 6.0)
        byte = np.where(mant > 0.5, ex, ex - 1) + 127
    byte = np.clip(np.where(amax > 0, byte, 1), 1, 254)
    scaled = (w * np.exp2(127.0 - byte)[:, None, :]).reshape(k, n).astype(np.float32)
    by_word = np.ascontiguousarray(scaled.reshape(k // 512, 128, 4, n).transpose(0, 1, 3, 2))
    if fmt == "e4m3":
        words = by_word.astype(ml_dtypes.float8_e4m3fn).view(np.uint8)
    else:
        c = by_word.astype(ml_dtypes.float4_e2m1fn).view(np.uint8) & 0xF
        words = (c[..., 0::2] | (c[..., 1::2] << 4)).reshape(k // 512, 128, 2 * n)
    return np.ascontiguousarray(words), np.ascontiguousarray(byte.astype(np.uint8).reshape(k // 512, 16, n))


def unpack_weight(words, scales, fmt):
    g, _, n = scales.shape
    words = np.ascontiguousarray(words).reshape(g, 128, n, -1)
    if fmt == "e4m3":
        vals = words.view(ml_dtypes.float8_e4m3fn).astype(np.float64)
    else:
        nib = np.empty((g, 128, n, 4), np.uint8)
        nib[..., 0::2] = words & 0xF
        nib[..., 1::2] = words >> 4
        vals = E2M1[nib]
    vals = vals * np.repeat(np.exp2(scales.astype(np.float64) - 127.0), 8, axis=1)[..., None]
    return vals.transpose(0, 1, 3, 2).reshape(g * 512, n)


B, N, T, D, NQ = 1, 512, 2048, 1024, 256


def setup_inputs():
    n = np.random.standard_normal
    idx = np.random.permutation(T)[:B * N]
    s = mx_kscale(D)[:, None]
    mid = n((D, T))
    kp = pack_weight((mid + np.abs(n((D, T)))) / s, "e2m1")
    cp = pack_weight((mid - np.abs(n((D, T)))) / s, "e2m1")
    return {
        "qT": (n((B, D, NQ)) * s * (1.00 / np.sqrt(D))).astype(np.float32),
        "k_words": np.ascontiguousarray(kp[0].reshape(1, 2, 128, T, 2).transpose(0, 2, 3, 1, 4)).reshape(1, 128, T, 4),
        "k_scales": kp[1],
        "c_words": np.ascontiguousarray(cp[0].reshape(1, 2, 128, T, 2).transpose(0, 2, 3, 1, 4)).reshape(1, 128, T, 4),
        "c_scales": cp[1],
        "offs": striped(idx),
    }


def reference(qT, k_words, k_scales, c_words, c_scales, offs):
    idx = unstriped(offs)
    pick = lambda x, which: x[:, which].reshape(x.shape[0], B, -1).transpose(1, 0, 2)
    k = unpack_weight(k_words.reshape(1, 128, T, 2, 2).transpose(0, 3, 1, 2, 4).reshape(2, 128, 2 * T), k_scales, "e2m1")
    kg = pick(k, idx)
    c = unpack_weight(c_words.reshape(1, 128, T, 2, 2).transpose(0, 3, 1, 2, 4).reshape(2, 128, 2 * T), c_scales, "e2m1")
    cg = pick(c, idx)
    hiq = mxq(np.maximum(f64(qT), 0.0), 1, "e4m3")
    loq = mxq(np.minimum(f64(qT), 0.0), 1, "e4m3")
    a = (hiq.transpose(0, 2, 1) @ kg) + (loq.transpose(0, 2, 1) @ cg)
    return a

@@ -1,0 +1,130 @@
+from contextlib import ExitStack
+
+import concourse.mybir as mybir
+
+D, T, N, NQ = 1024, 2048, 512, 256
+FLOPS = 2 * 2 * D * N * NQ
+
+F32 = mybir.dt.float32
+BF16 = mybir.dt.bfloat16
+I32 = mybir.dt.int32
+U32 = mybir.dt.uint32
+U16 = mybir.dt.uint16
+U8 = mybir.dt.uint8
+FP8X4 = mybir.dt.float8_e4m3fn_x4
+FP4X4 = mybir.dt.float4_e2m1fn_x4
+RELU = mybir.ActivationFunctionType.Relu
+
+P = 128
+PACK = 4
+PASSES = 2
+HALF = N // 2
+NB = 128
+
+
+def tile_attend_quest_topk_kernel(tc, qT, k_words, k_scales, c_words, c_scales, offs, out):
+    nc = tc.nc
+    with ExitStack() as ctx:
+        keep = ctx.enter_context(tc.tile_pool(name="keep", bufs=1))
+        psum = ctx.enter_context(tc.psum_pool(name="psum", bufs=1))
+
+        offsets = keep.tile([P, N // 16], U16, name="offsets")
+        nc.sync.dma_start(offsets[:], offs)
+
+        scale_win = []
+        for name, scales in (("k", k_scales), ("c", c_scales)):
+            win = keep.tile([P, T], U8, name=name + "_scale_win", align_bytes=64)
+            nc.scalar.dma_start(win[96:128, :].bitcast(I32), scales.bitcast(I32).rearrange("o f w -> f o w"))
+            nc.vector.memset(win[0:96, :].bitcast(I32), 0)
+            scale_win.append(win)
+        planes = keep.tile([P, PASSES * 2 * N], U8, name="planes", align_bytes=64)
+        nc.vector.memset(planes[:].bitcast(I32), 0)
+
+        q_raw = [keep.tile([P, PACK, NQ], F32, name="q_raw%d" % o, align_bytes=64) for o in range(PASSES)]
+        word_win = [keep.tile([P, T], I32, name=name + "_word_win", align_bytes=64) for name in ("k", "c")]
+
+        def load_q(o):
+            nc.scalar.dma_start(q_raw[o][:], qT[0, 512 * o : 512 * (o + 1), :].rearrange("(p t) m -> p t m", t=PACK))
+
+        def load_words(s, words):
+            nc.scalar.dma_start(word_win[s][:], words[0].rearrange("p t b -> p (t b)").bitcast(I32))
+
+        load_q(0)
+        load_words(0, k_words)
+        load_q(1)
+        load_words(1, c_words)
+
+        got_scales = keep.tile([P, 2 * N], U8, name="got_scales", align_bytes=64)
+        for s in range(2):
+            nc.vector.tensor_copy(got_scales[:, s * N : (s + 1) * N], scale_win[s][:].indirect(offsets[:]))
+        for quad in range(4):
+            nc.sync.dma_start(
+                planes[32 * quad : 32 * quad + 4, :].bitcast(I32).rearrange("p (o w) -> p o w", o=PASSES),
+                got_scales[96 + 8 * quad : 96 + 8 * quad + 8, :].bitcast(I32),
+            )
+
+        q_codes, q_scales = {}, {}
+
+        def quantise_q(o):
+            src = q_raw[o][:].rearrange("p t (c i) -> p c t i", i=4)
+            parts = [keep.tile([P, NQ * PACK], BF16, name="q_part%d_%d" % (s, o), align_bytes=64) for s in range(2)]
+            views = [part[:].rearrange("p (c i t) -> p c t i", i=4, t=PACK) for part in parts]
+            nc.scalar.activation(views[0], src, RELU)
+            nc.vector.tensor_scalar_min(views[1], src, 0.0)
+            for s in range(2):
+                q_codes[s, o] = keep.tile([P, NQ], U32, name="q_codes%d_%d" % (s, o), align_bytes=64)
+                q_scales[s, o] = keep.tile([P, NQ], U8, name="q_scales%d_%d" % (s, o), align_bytes=64)
+                nc.vector.quantize_mx(out=q_codes[s, o][:].bitcast(FP8X4), scales=q_scales[s, o][:], in_=parts[s][:])
+
+        words16 = {}
+
+        def gather_words(s):
+            got = [keep.tile([P, HALF], U32, name="got_words%d_%d" % (s, h), align_bytes=64) for h in range(2)]
+            for h in range(2):
+                lists = offsets[:, h * (HALF // 16) : (h + 1) * (HALF // 16)]
+                nc.vector.tensor_copy(got[h][:], word_win[s][:].bitcast(U32).indirect(lists))
+            for h in range(2):
+                words16[s, h] = keep.tile([P, PASSES * HALF], U16, name="words16_%d_%d" % (s, h), align_bytes=64)
+                nc.vector.tensor_copy(
+                    words16[s, h][:].rearrange("p (o n) -> p o n", o=PASSES),
+                    got[h][:].bitcast(U16).rearrange("p (n o) -> p o n", o=PASSES),
+                )
+
+        banks = {(m, b): psum.tile([P, NB], F32, name="bank%d_%d" % (m, b)) for m in range(2) for b in range(N // NB)}
+
+        def multiply(s, o, m, b):
+            h, n0 = divmod(b * NB, HALF)
+            plane0 = (o * 2 + s) * N + b * NB
+            nc.tensor.matmul_mx(
+                out=banks[m, b][:],
+                lhsT=q_codes[s, o][:, m * P : (m + 1) * P].bitcast(FP8X4),
+                lhsT_scale=q_scales[s, o][:, m * P : (m + 1) * P],
+                rhs=words16[s, h][:, o * HALF + n0 : o * HALF + n0 + NB].bitcast(FP4X4),
+                rhs_scale=planes[:, plane0 : plane0 + NB],
+                start=(s == 0 and o == 0),
+                stop=(s == 1 and o == PASSES - 1),
+            )
+
+        quantise_q(0)
+        gather_words(0)
+        quantise_q(1)
+        for o in range(PASSES):
+            for m in range(2):
+                for b in range(N // NB):
+                    multiply(0, o, m, b)
+        gather_words(1)
+
+        out_view = out[0].rearrange("(m p) n -> p m n", p=P)
+        for h in range(2):
+            staged = keep.tile([P, 2, HALF], F32, name="staged%d" % h, align_bytes=64)
+            for j in range(2):
+                b = 2 * h + j
+                for m in range(2):
+                    for o in range(PASSES):
+                        multiply(1, o, m, b)
+                    dst = staged[:, m, j * NB : (j + 1) * NB]
+                    if m == 0 or h == 0:
+                        nc.scalar.copy(dst, banks[m, b][:])
+                    else:
+                        nc.vector.tensor_copy(dst, banks[m, b][:])
+            nc.sync.dma_start(out_view[:, :, h * HALF : (h + 1) * HALF], staged[:])

@@ -26,6 +26,8 @@ def tile_attend_quest_topk_kernel(tc, qT, k_words, k_scales, c_words, c_scales, 
     nc = tc.nc
     with ExitStack() as ctx:
         keep = ctx.enter_context(tc.tile_pool(name="keep", bufs=1))
+        late = ctx.enter_context(tc.tile_pool(name="late", bufs=1))
+        reuse = ctx.enter_context(tc.tile_pool(name="reuse", bufs=1))
         psum = ctx.enter_context(tc.psum_pool(name="psum", bufs=1))
 
         offsets = keep.tile([P, N // 16], U16, name="offsets")
@@ -33,26 +35,24 @@ def tile_attend_quest_topk_kernel(tc, qT, k_words, k_scales, c_words, c_scales, 
 
         scale_win = []
         for name, scales in (("k", k_scales), ("c", c_scales)):
-            win = keep.tile([P, T], U8, name=name + "_scale_win", align_bytes=64)
+            win = keep.tile([P, T], U8, name=name + "_scale_win", tag=name + "_stage", align_bytes=64)
             nc.scalar.dma_start(win[96:128, :].bitcast(I32), scales.bitcast(I32).rearrange("o f w -> f o w"))
             nc.vector.memset(win[0:96, :].bitcast(I32), 0)
             scale_win.append(win)
         planes = keep.tile([P, PASSES * 2 * N], U8, name="planes", align_bytes=64)
         nc.vector.memset(planes[:].bitcast(I32), 0)
 
-        q_raw = [keep.tile([P, PACK, NQ], F32, name="q_raw%d" % o, align_bytes=64) for o in range(PASSES)]
-        word_win = [keep.tile([P, T], I32, name=name + "_word_win", align_bytes=64) for name in ("k", "c")]
+        def load_q(o, queue, tag):
+            raw = keep.tile([P, PACK, NQ], F32, name="q_raw%d" % o, tag=tag, align_bytes=64)
+            queue.dma_start(raw[:], qT[0, 512 * o : 512 * (o + 1), :].rearrange("(p t) m -> p t m", t=PACK))
+            return raw
 
-        def load_q(o):
-            nc.scalar.dma_start(q_raw[o][:], qT[0, 512 * o : 512 * (o + 1), :].rearrange("(p t) m -> p t m", t=PACK))
-
-        def load_words(s, words):
-            nc.scalar.dma_start(word_win[s][:], words[0].rearrange("p t b -> p (t b)").bitcast(I32))
-
-        load_q(0)
-        load_words(0, k_words)
-        load_q(1)
-        load_words(1, c_words)
+        q_raw0 = load_q(0, nc.scalar, "q_stage")
+        word_win = []
+        word_win.append(keep.tile([P, T], I32, name="k_word_win", align_bytes=64))
+        word_win.append(late.tile([P, T], I32, name="c_word_win", offset=0, align_bytes=64))
+        for win, words in zip(word_win, (k_words, c_words)):
+            nc.scalar.dma_start(win[:], words[0].rearrange("p t b -> p (t b)").bitcast(I32))
 
         got_scales = keep.tile([P, 2 * N], U8, name="got_scales", align_bytes=64)
         for s in range(2):
@@ -62,69 +62,79 @@ def tile_attend_quest_topk_kernel(tc, qT, k_words, k_scales, c_words, c_scales, 
                 planes[32 * quad : 32 * quad + 4, :].bitcast(I32).rearrange("p (o w) -> p o w", o=PASSES),
                 got_scales[96 + 8 * quad : 96 + 8 * quad + 8, :].bitcast(I32),
             )
+        q_raw1 = load_q(1, nc.sync, "c_stage")
 
         q_codes, q_scales = {}, {}
 
-        def quantise_q(o):
-            src = q_raw[o][:].rearrange("p t (c i) -> p c t i", i=4)
-            parts = [keep.tile([P, NQ * PACK], BF16, name="q_part%d_%d" % (s, o), align_bytes=64) for s in range(2)]
+        def quantise_q(o, raw, m0, rows, parts, code_tiles):
+            src = raw[:, :, m0 : m0 + rows].rearrange("p t (c i) -> p c t i", i=4)
             views = [part[:].rearrange("p (c i t) -> p c t i", i=4, t=PACK) for part in parts]
             nc.scalar.activation(views[0], src, RELU)
             nc.vector.tensor_scalar_min(views[1], src, 0.0)
             for s in range(2):
-                q_codes[s, o] = keep.tile([P, NQ], U32, name="q_codes%d_%d" % (s, o), align_bytes=64)
-                q_scales[s, o] = keep.tile([P, NQ], U8, name="q_scales%d_%d" % (s, o), align_bytes=64)
-                nc.vector.quantize_mx(out=q_codes[s, o][:].bitcast(FP8X4), scales=q_scales[s, o][:], in_=parts[s][:])
+                codes = code_tiles[s]
+                scales = keep.tile([P, rows], U8, name="q_scales%d_%d_%d" % (s, o, m0), align_bytes=64)
+                nc.vector.quantize_mx(out=codes[:].bitcast(FP8X4), scales=scales[:], in_=parts[s][:])
+                for j in range(rows // P):
+                    q_codes[s, o, m0 // P + j] = codes[:, j * P : (j + 1) * P]
+                    q_scales[s, o, m0 // P + j] = scales[:, j * P : (j + 1) * P]
 
         words16 = {}
 
         def gather_words(s):
-            got = [keep.tile([P, HALF], U32, name="got_words%d_%d" % (s, h), align_bytes=64) for h in range(2)]
+            got = [reuse.tile([P, HALF], U32, name="got_words%d_%d" % (s, h), offset=1024 * h, align_bytes=64) for h in range(2)]
             for h in range(2):
                 lists = offsets[:, h * (HALF // 16) : (h + 1) * (HALF // 16)]
                 nc.vector.tensor_copy(got[h][:], word_win[s][:].bitcast(U32).indirect(lists))
             for h in range(2):
-                words16[s, h] = keep.tile([P, PASSES * HALF], U16, name="words16_%d_%d" % (s, h), align_bytes=64)
+                parted = keep.tile([P, PASSES * HALF], U16, name="words16_%d_%d" % (s, h), align_bytes=64)
                 nc.vector.tensor_copy(
-                    words16[s, h][:].rearrange("p (o n) -> p o n", o=PASSES),
+                    parted[:].rearrange("p (o n) -> p o n", o=PASSES),
                     got[h][:].bitcast(U16).rearrange("p (n o) -> p o n", o=PASSES),
                 )
+                for o in range(PASSES):
+                    for j in range(HALF // NB):
+                        words16[s, o, h * (HALF // NB) + j] = parted[:, o * HALF + j * NB : o * HALF + (j + 1) * NB]
 
         banks = {(m, b): psum.tile([P, NB], F32, name="bank%d_%d" % (m, b)) for m in range(2) for b in range(N // NB)}
 
         def multiply(s, o, m, b):
-            h, n0 = divmod(b * NB, HALF)
             plane0 = (o * 2 + s) * N + b * NB
             nc.tensor.matmul_mx(
                 out=banks[m, b][:],
-                lhsT=q_codes[s, o][:, m * P : (m + 1) * P].bitcast(FP8X4),
-                lhsT_scale=q_scales[s, o][:, m * P : (m + 1) * P],
-                rhs=words16[s, h][:, o * HALF + n0 : o * HALF + n0 + NB].bitcast(FP4X4),
+                lhsT=q_codes[s, o, m].bitcast(FP8X4),
+                lhsT_scale=q_scales[s, o, m],
+                rhs=words16[s, o, b].bitcast(FP4X4),
                 rhs_scale=planes[:, plane0 : plane0 + NB],
                 start=(s == 0 and o == 0),
                 stop=(s == 1 and o == PASSES - 1),
             )
 
-        quantise_q(0)
-        gather_words(0)
-        quantise_q(1)
-        for o in range(PASSES):
-            for m in range(2):
-                for b in range(N // NB):
-                    multiply(0, o, m, b)
-        gather_words(1)
-
-        out_view = out[0].rearrange("(m p) n -> p m n", p=P)
-        for h in range(2):
-            staged = keep.tile([P, 2, HALF], F32, name="staged%d" % h, align_bytes=64)
-            for j in range(2):
-                b = 2 * h + j
+        hi0 = reuse.tile([P, NQ * PACK], BF16, name="hi0", offset=0, align_bytes=64)
+        lo0 = keep.tile([P, NQ * PACK], BF16, name="lo0", align_bytes=64)
+        codes0 = [keep.tile([P, NQ], U32, name="codes0_%d" % s, align_bytes=64) for s in range(2)]
+        quantise_q(0, q_raw0, 0, NQ, (hi0, lo0), codes0)
+        for s in range(2):
+            gather_words(s)
+            for b in range(N // NB):
                 for m in range(2):
-                    for o in range(PASSES):
-                        multiply(1, o, m, b)
-                    dst = staged[:, m, j * NB : (j + 1) * NB]
-                    if m == 0 or h == 0:
-                        nc.scalar.copy(dst, banks[m, b][:])
+                    multiply(s, 0, m, b)
+
+        for m in range(2):
+            hi1 = keep.tile([P, P * PACK], BF16, name="hi1_%d" % m, align_bytes=64)
+            lo1 = late.tile([P, P * PACK], BF16, name="lo1_%d" % m, offset=2048 * m, align_bytes=64)
+            codes1 = [late.tile([P, P], U32, name="codes1_%d_%d" % (s, m), offset=2048 * m + 1024 + 512 * s, align_bytes=64) for s in range(2)]
+            quantise_q(1, q_raw1, m * P, P, (hi1, lo1), codes1)
+        for m in range(2):
+            for s in range(2):
+                for b in range(N // NB):
+                    multiply(s, 1, m, b)
+            for h in range(2):
+                staged = keep.tile([P, HALF], F32, name="staged%d_%d" % (m, h), align_bytes=64)
+                for j in range(2):
+                    dst = staged[:, j * NB : (j + 1) * NB]
+                    if m == 0 or j == 0:
+                        nc.scalar.copy(dst, banks[m, 2 * h + j][:])
                     else:
-                        nc.vector.tensor_copy(dst, banks[m, b][:])
-            nc.sync.dma_start(out_view[:, :, h * HALF : (h + 1) * HALF], staged[:])
+                        nc.vector.tensor_copy(dst, banks[m, 2 * h + j][:])
+                nc.sync.dma_start(out[0, m * P : (m + 1) * P, h * HALF : (h + 1) * HALF], staged[:])

@@ -86,6 +86,18 @@ def tile_attend_quest_topk_kernel(tc, qT, k_words, k_scales, c_words, c_scales, 
             for h in range(2):
                 lists = offsets[:, h * (HALF // 16) : (h + 1) * (HALF // 16)]
                 nc.vector.tensor_copy(got[h][:], word_win[s][:].bitcast(U32).indirect(lists))
+            if s == 0:
+                warm = psum.tile([P, N], F32, name="warm", tag="bank1_3")
+                for m in range(2):
+                    nc.tensor.matmul_mx(
+                        out=warm[:],
+                        lhsT=q_codes[0, 0, m].bitcast(FP8X4),
+                        lhsT_scale=q_scales[0, 0, m],
+                        rhs=got[0][:].bitcast(U16).bitcast(FP4X4),
+                        rhs_scale=got_scales[:, 0:N],
+                        start=True,
+                        stop=True,
+                    )
             for h in range(2):
                 parted = keep.tile([P, PASSES * HALF], U16, name="words16_%d_%d" % (s, h), align_bytes=64)
                 nc.vector.tensor_copy(
@@ -96,9 +108,11 @@ def tile_attend_quest_topk_kernel(tc, qT, k_words, k_scales, c_words, c_scales, 
                     for j in range(HALF // NB):
                         words16[s, o, h * (HALF // NB) + j] = parted[:, o * HALF + j * NB : o * HALF + (j + 1) * NB]
 
-        banks = {(m, b): psum.tile([P, NB], F32, name="bank%d_%d" % (m, b)) for m in range(2) for b in range(N // NB)}
+        banks = {}
 
         def multiply(s, o, m, b):
+            if (m, b) not in banks:
+                banks.setdefault((m, b), psum.tile([P, NB], F32, name="bank%d_%d" % (m, b), tag="bank%d_%d" % (m, b)))
             plane0 = (o * 2 + s) * N + b * NB
             nc.tensor.matmul_mx(
                 out=banks[m, b][:],

@@ -80,6 +80,18 @@ def tile_attend_quest_topk_kernel(tc, qT, k_words, k_scales, c_words, c_scales, 
                     q_scales[s, o, m0 // P + j] = scales[:, j * P : (j + 1) * P]
 
         words16 = {}
+        warm = psum.tile([P, N], F32, name="warm", tag="bank0_0")
+
+        def warm_up(m, words):
+            nc.tensor.matmul_mx(
+                out=warm[:],
+                lhsT=q_codes[0, 0, m].bitcast(FP8X4),
+                lhsT_scale=q_scales[0, 0, m],
+                rhs=words.bitcast(FP4X4),
+                rhs_scale=got_scales[:, 0:N],
+                start=True,
+                stop=True,
+            )
 
         def gather_words(s):
             got = [reuse.tile([P, HALF], U32, name="got_words%d_%d" % (s, h), offset=1024 * h, align_bytes=64) for h in range(2)]
@@ -87,23 +99,15 @@ def tile_attend_quest_topk_kernel(tc, qT, k_words, k_scales, c_words, c_scales, 
                 lists = offsets[:, h * (HALF // 16) : (h + 1) * (HALF // 16)]
                 nc.vector.tensor_copy(got[h][:], word_win[s][:].bitcast(U32).indirect(lists))
             if s == 0:
-                warm = psum.tile([P, N], F32, name="warm", tag="bank1_3")
-                for m in range(2):
-                    nc.tensor.matmul_mx(
-                        out=warm[:],
-                        lhsT=q_codes[0, 0, m].bitcast(FP8X4),
-                        lhsT_scale=q_scales[0, 0, m],
-                        rhs=got[0][:].bitcast(U16).bitcast(FP4X4),
-                        rhs_scale=got_scales[:, 0:N],
-                        start=True,
-                        stop=True,
-                    )
+                warm_up(0, got[0][:].bitcast(U16))
             for h in range(2):
                 parted = keep.tile([P, PASSES * HALF], U16, name="words16_%d_%d" % (s, h), align_bytes=64)
                 nc.vector.tensor_copy(
                     parted[:].rearrange("p (o n) -> p o n", o=PASSES),
                     got[h][:].bitcast(U16).rearrange("p (n o) -> p o n", o=PASSES),
                 )
+                if s == 0 and h == 0:
+                    warm_up(1, parted[:])
                 for o in range(PASSES):
                     for j in range(HALF // NB):
                         words16[s, o, h * (HALF // NB) + j] = parted[:, o * HALF + j * NB : o * HALF + (j + 1) * NB]

@@ -66,18 +66,24 @@ def tile_attend_quest_topk_kernel(tc, qT, k_words, k_scales, c_words, c_scales, 
 
         q_codes, q_scales = {}, {}
 
-        def quantise_q(o, raw, m0, rows, parts, code_tiles):
+        def views(raw, m0, rows, part):
             src = raw[:, :, m0 : m0 + rows].rearrange("p t (c i) -> p c t i", i=4)
-            views = [part[:].rearrange("p (c i t) -> p c t i", i=4, t=PACK) for part in parts]
-            nc.scalar.activation(views[0], src, RELU)
-            nc.vector.tensor_scalar_min(views[1], src, 0.0)
-            for s in range(2):
-                codes = code_tiles[s]
-                scales = keep.tile([P, rows], U8, name="q_scales%d_%d_%d" % (s, o, m0), align_bytes=64)
-                nc.vector.quantize_mx(out=codes[:].bitcast(FP8X4), scales=scales[:], in_=parts[s][:])
-                for j in range(rows // P):
-                    q_codes[s, o, m0 // P + j] = codes[:, j * P : (j + 1) * P]
-                    q_scales[s, o, m0 // P + j] = scales[:, j * P : (j + 1) * P]
+            return part[:].rearrange("p (c i t) -> p c t i", i=4, t=PACK), src
+
+        def positive_part(raw, m0, rows, part):
+            dst, src = views(raw, m0, rows, part)
+            nc.scalar.activation(dst, src, RELU)
+
+        def negative_part(raw, m0, rows, part):
+            dst, src = views(raw, m0, rows, part)
+            nc.vector.tensor_scalar_min(dst, src, 0.0)
+
+        def quantise(s, o, m0, rows, part, codes):
+            scales = keep.tile([P, rows], U8, name="q_scales%d_%d_%d" % (s, o, m0), align_bytes=64)
+            nc.vector.quantize_mx(out=codes[:].bitcast(FP8X4), scales=scales[:], in_=part[:])
+            for j in range(rows // P):
+                q_codes[s, o, m0 // P + j] = codes[:, j * P : (j + 1) * P]
+                q_scales[s, o, m0 // P + j] = scales[:, j * P : (j + 1) * P]
 
         words16 = {}
         warm = psum.tile([P, N], F32, name="warm", tag="bank0_0")
@@ -94,23 +100,24 @@ def tile_attend_quest_topk_kernel(tc, qT, k_words, k_scales, c_words, c_scales, 
             )
 
         def gather_words(s):
-            got = [reuse.tile([P, HALF], U32, name="got_words%d_%d" % (s, h), offset=1024 * h, align_bytes=64) for h in range(2)]
+            got = [reuse.tile([P, HALF], U32, name="got_words%d_%d" % (s, h), offset=((1024, 0), (1536, 2560))[s][h], align_bytes=64) for h in range(2)]
             for h in range(2):
                 lists = offsets[:, h * (HALF // 16) : (h + 1) * (HALF // 16)]
                 nc.vector.tensor_copy(got[h][:], word_win[s][:].bitcast(U32).indirect(lists))
-            if s == 0:
-                warm_up(0, got[0][:].bitcast(U16))
-            for h in range(2):
-                parted = keep.tile([P, PASSES * HALF], U16, name="words16_%d_%d" % (s, h), align_bytes=64)
-                nc.vector.tensor_copy(
-                    parted[:].rearrange("p (o n) -> p o n", o=PASSES),
-                    got[h][:].bitcast(U16).rearrange("p (n o) -> p o n", o=PASSES),
-                )
-                if s == 0 and h == 0:
-                    warm_up(1, parted[:])
-                for o in range(PASSES):
-                    for j in range(HALF // NB):
-                        words16[s, o, h * (HALF // NB) + j] = parted[:, o * HALF + j * NB : o * HALF + (j + 1) * NB]
+            return got
+
+        def part_words(s, got, b0, blocks):
+            width = blocks * NB
+            parted = keep.tile([P, PASSES * width], U16, name="words16_%d_%d" % (s, b0), align_bytes=64)
+            c0 = (b0 % 2) * NB
+            nc.vector.tensor_copy(
+                parted[:].rearrange("p (o n) -> p o n", o=PASSES),
+                got[b0 // 2][:, c0 : c0 + width].bitcast(U16).rearrange("p (n o) -> p o n", o=PASSES),
+            )
+            for o in range(PASSES):
+                for j in range(blocks):
+                    words16[s, o, b0 + j] = parted[:, o * width + j * NB : o * width + (j + 1) * NB]
+            return parted
 
         banks = {}
 
@@ -129,30 +136,62 @@ def tile_attend_quest_topk_kernel(tc, qT, k_words, k_scales, c_words, c_scales, 
             )
 
         hi0 = reuse.tile([P, NQ * PACK], BF16, name="hi0", offset=0, align_bytes=64)
-        lo0 = keep.tile([P, NQ * PACK], BF16, name="lo0", align_bytes=64)
-        codes0 = [keep.tile([P, NQ], U32, name="codes0_%d" % s, align_bytes=64) for s in range(2)]
-        quantise_q(0, q_raw0, 0, NQ, (hi0, lo0), codes0)
-        for s in range(2):
-            gather_words(s)
-            for b in range(N // NB):
+        lo0 = reuse.tile([P, NQ * PACK], BF16, name="lo0", offset=2048, align_bytes=64)
+        positive_part(q_raw0, 0, NQ, hi0)
+        flipped = reuse.tile([P, NQ * PACK], BF16, name="flipped", offset=4096, align_bytes=64)
+        dst, src = views(q_raw0, 0, NQ, flipped)
+        nc.scalar.activation(dst, src, RELU, scale=-1.0)
+        nc.scalar.activation(lo0[:], flipped[:], mybir.ActivationFunctionType.Copy, scale=-1.0)
+        quantise(0, 0, 0, NQ, hi0, keep.tile([P, NQ], U32, name="codes0_0", align_bytes=64))
+        got = gather_words(0)
+        warm_up(0, got[0][:].bitcast(U16))
+        warm_up(1, part_words(0, got, 0, 2)[:])
+        quantise(1, 0, 0, NQ, lo0, keep.tile([P, NQ], U32, name="codes0_1", align_bytes=64))
+        part_words(0, got, 2, 2)
+        for b in range(N // NB):
+            for m in range(2):
+                multiply(0, 0, m, b)
+        got = gather_words(1)
+        for b0, blocks in [[0,2],[2,2]]:
+            part_words(1, got, b0, blocks)
+            for b in range(b0, b0 + blocks):
                 for m in range(2):
-                    multiply(s, 0, m, b)
+                    multiply(1, 0, m, b)
 
+        hi1 = [reuse.tile([P, P * PACK], BF16, name="hi1_%d" % m, offset=4096 + 1024 * m, align_bytes=64) for m in range(2)]
+        lo1 = [late.tile([P, P * PACK], BF16, name="lo1_%d" % m, offset=2048 * m, align_bytes=64) for m in range(2)]
+        codes1 = {
+            (s, m): late.tile([P, P], U32, name="codes1_%d_%d" % (s, m), offset=2048 * m + 1024 + 512 * s, align_bytes=64)
+            for s in range(2)
+            for m in range(2)
+        }
         for m in range(2):
-            hi1 = keep.tile([P, P * PACK], BF16, name="hi1_%d" % m, align_bytes=64)
-            lo1 = late.tile([P, P * PACK], BF16, name="lo1_%d" % m, offset=2048 * m, align_bytes=64)
-            codes1 = [late.tile([P, P], U32, name="codes1_%d_%d" % (s, m), offset=2048 * m + 1024 + 512 * s, align_bytes=64) for s in range(2)]
-            quantise_q(1, q_raw1, m * P, P, (hi1, lo1), codes1)
-        for m in range(2):
-            for s in range(2):
-                for b in range(N // NB):
-                    multiply(s, 1, m, b)
-            for h in range(2):
-                staged = keep.tile([P, HALF], F32, name="staged%d_%d" % (m, h), align_bytes=64)
-                for j in range(2):
-                    dst = staged[:, j * NB : (j + 1) * NB]
-                    if m == 0 or j == 0:
-                        nc.scalar.copy(dst, banks[m, 2 * h + j][:])
-                    else:
-                        nc.vector.tensor_copy(dst, banks[m, 2 * h + j][:])
-                nc.sync.dma_start(out[0, m * P : (m + 1) * P, h * HALF : (h + 1) * HALF], staged[:])
+            positive_part(q_raw1, m * P, P, hi1[m])
+
+        def products(s, m):
+            for b in range(N // NB):
+                multiply(s, 1, m, b)
+
+        copiers = {"S": nc.scalar.copy, "V": nc.vector.tensor_copy}
+        queues = {"sync": nc.sync, "scalar": nc.scalar}
+
+        def leave(m):
+            for mm, b0, blocks, queue in [[0,0,2,"sync"],[0,2,2,"sync"],[1,0,2,"sync"],[1,2,2,"sync"]]:
+                if mm == m:
+                    staged = keep.tile([P, blocks * NB], F32, name="staged%d_%d" % (m, b0), align_bytes=64)
+                    for j in range(blocks):
+                        copiers[["SSSS","SVSV"][m][b0 + j]](staged[:, j * NB : (j + 1) * NB], banks[m, b0 + j][:])
+                    queues[queue].dma_start(out[0, m * P : (m + 1) * P, b0 * NB : (b0 + blocks) * NB], staged[:])
+
+        negative_part(q_raw1, 0, P, lo1[0])
+        quantise(0, 1, 0, P, hi1[0], codes1[0, 0])
+        products(0, 0)
+        quantise(1, 1, 0, P, lo1[0], codes1[1, 0])
+        products(1, 0)
+        leave(0)
+        negative_part(q_raw1, P, P, lo1[1])
+        quantise(0, 1, P, P, hi1[1], codes1[0, 1])
+        products(0, 1)
+        quantise(1, 1, P, P, lo1[1], codes1[1, 1])
+        products(1, 1)
+        leave(1)

@@ -86,18 +86,6 @@ def tile_attend_quest_topk_kernel(tc, qT, k_words, k_scales, c_words, c_scales, 
                 q_scales[s, o, m0 // P + j] = scales[:, j * P : (j + 1) * P]
 
         words16 = {}
-        warm = psum.tile([P, N], F32, name="warm", tag="bank0_0")
-
-        def warm_up(m, words):
-            nc.tensor.matmul_mx(
-                out=warm[:],
-                lhsT=q_codes[0, 0, m].bitcast(FP8X4),
-                lhsT_scale=q_scales[0, 0, m],
-                rhs=words.bitcast(FP4X4),
-                rhs_scale=got_scales[:, 0:N],
-                start=True,
-                stop=True,
-            )
 
         def gather_words(s):
             got = [reuse.tile([P, HALF], U32, name="got_words%d_%d" % (s, h), offset=((1024, 0), (1536, 2560))[s][h], align_bytes=64) for h in range(2)]
@@ -144,8 +132,7 @@ def tile_attend_quest_topk_kernel(tc, qT, k_words, k_scales, c_words, c_scales, 
         nc.scalar.activation(lo0[:], flipped[:], mybir.ActivationFunctionType.Copy, scale=-1.0)
         quantise(0, 0, 0, NQ, hi0, keep.tile([P, NQ], U32, name="codes0_0", align_bytes=64))
         got = gather_words(0)
-        warm_up(0, got[0][:].bitcast(U16))
-        warm_up(1, part_words(0, got, 0, 2)[:])
+        part_words(0, got, 0, 2)
         quantise(1, 0, 0, NQ, lo0, keep.tile([P, NQ], U32, name="codes0_1", align_bytes=64))
         part_words(0, got, 2, 2)
         for b in range(N // NB):

@@ -62,9 +62,13 @@ def tile_attend_quest_topk_kernel(tc, qT, k_words, k_scales, c_words, c_scales, 
                 planes[32 * quad : 32 * quad + 4, :].bitcast(I32).rearrange("p (o w) -> p o w", o=PASSES),
                 got_scales[96 + 8 * quad : 96 + 8 * quad + 8, :].bitcast(I32),
             )
-        q_raw1 = load_q(1, nc.sync, "c_stage")
+        q_rows1 = qT[0, 512:1024, :].rearrange("(p t) m -> p (t m)", t=PACK)
+        q_flat1 = keep.tile([P, PACK * NQ], F32, name="q_raw1", tag="c_stage", align_bytes=64)
+        for u in range(2):
+            nc.sync.dma_start(q_flat1[:, 2 * u * NQ : 2 * (u + 1) * NQ], q_rows1[:, 2 * u * NQ : 2 * (u + 1) * NQ])
+        q_raw1 = q_flat1[:].rearrange("p (t m) -> p t m", t=PACK)
 
-        q_codes, q_scales = {}, {}
+        q_codes, q_scales, scale_tiles = {}, {}, {}
 
         def views(raw, m0, rows, part):
             src = raw[:, :, m0 : m0 + rows].rearrange("p t (c i) -> p c t i", i=4)
@@ -81,6 +85,7 @@ def tile_attend_quest_topk_kernel(tc, qT, k_words, k_scales, c_words, c_scales, 
         def quantise(s, o, m0, rows, part, codes):
             scales = keep.tile([P, rows], U8, name="q_scales%d_%d_%d" % (s, o, m0), align_bytes=64)
             nc.vector.quantize_mx(out=codes[:].bitcast(FP8X4), scales=scales[:], in_=part[:])
+            scale_tiles.setdefault((s, o, m0), scales)
             for j in range(rows // P):
                 q_codes[s, o, m0 // P + j] = codes[:, j * P : (j + 1) * P]
                 q_scales[s, o, m0 // P + j] = scales[:, j * P : (j + 1) * P]
@@ -132,6 +137,17 @@ def tile_attend_quest_topk_kernel(tc, qT, k_words, k_scales, c_words, c_scales, 
         nc.scalar.activation(lo0[:], flipped[:], mybir.ActivationFunctionType.Copy, scale=-1.0)
         quantise(0, 0, 0, NQ, hi0, keep.tile([P, NQ], U32, name="codes0_0", align_bytes=64))
         got = gather_words(0)
+        warm = psum.tile([P, HALF], F32, name="warm", tag="bank0_0")
+        for j in range(3):
+            nc.tensor.matmul_mx(
+                out=warm[:],
+                lhsT=q_codes[0, 0, 0].bitcast(FP8X4),
+                lhsT_scale=q_scales[0, 0, 0],
+                rhs=got[1][:].bitcast(U16)[:, (j % 2) * HALF : (j % 2 + 1) * HALF].bitcast(FP4X4),
+                rhs_scale=scale_tiles[0, 0, 0][:],
+                start=True,
+                stop=True,
+            )
         part_words(0, got, 0, 2)
         quantise(1, 0, 0, NQ, lo0, keep.tile([P, NQ], U32, name="codes0_1", align_bytes=64))
         part_words(0, got, 2, 2)
@@ -152,8 +168,10 @@ def tile_attend_quest_topk_kernel(tc, qT, k_words, k_scales, c_words, c_scales, 
             for s in range(2)
             for m in range(2)
         }
-        for m in range(2):
-            positive_part(q_raw1, m * P, P, hi1[m])
+        dst, src = views(q_raw1, 0, P, hi1[0])
+        for u in range(2):
+            nc.scalar.activation(dst[:, :, 2 * u : 2 * u + 2, :], src[:, :, 2 * u : 2 * u + 2, :], RELU)
+        positive_part(q_raw1, P, P, hi1[1])
 
         def products(s, m):
             for b in range(N // NB):

@@ -191,10 +191,11 @@ def tile_attend_quest_topk_kernel(tc, qT, k_words, k_scales, c_words, c_scales, 
         negative_part(q_raw1, 0, P, lo1[0])
         quantise(0, 1, 0, P, hi1[0], codes1[0, 0])
         products(0, 0)
+        negative_part(q_raw1, P, P // 2, lo1[1][:, 0 : P * PACK // 2])
         quantise(1, 1, 0, P, lo1[0], codes1[1, 0])
         products(1, 0)
         leave(0)
-        negative_part(q_raw1, P, P, lo1[1])
+        negative_part(q_raw1, P + P // 2, P // 2, lo1[1][:, P * PACK // 2 : P * PACK])
         quantise(0, 1, P, P, hi1[1], codes1[0, 1])
         products(0, 1)
         quantise(1, 1, P, P, lo1[1], codes1[1, 1])

@@ -68,7 +68,7 @@ def tile_attend_quest_topk_kernel(tc, qT, k_words, k_scales, c_words, c_scales, 
             nc.sync.dma_start(q_flat1[:, 2 * u * NQ : 2 * (u + 1) * NQ], q_rows1[:, 2 * u * NQ : 2 * (u + 1) * NQ])
         q_raw1 = q_flat1[:].rearrange("p (t m) -> p t m", t=PACK)
 
-        q_codes, q_scales, scale_tiles = {}, {}, {}
+        q_codes, q_scales = {}, {}
 
         def views(raw, m0, rows, part):
             src = raw[:, :, m0 : m0 + rows].rearrange("p t (c i) -> p c t i", i=4)
@@ -85,7 +85,6 @@ def tile_attend_quest_topk_kernel(tc, qT, k_words, k_scales, c_words, c_scales, 
         def quantise(s, o, m0, rows, part, codes):
             scales = keep.tile([P, rows], U8, name="q_scales%d_%d_%d" % (s, o, m0), align_bytes=64)
             nc.vector.quantize_mx(out=codes[:].bitcast(FP8X4), scales=scales[:], in_=part[:])
-            scale_tiles.setdefault((s, o, m0), scales)
             for j in range(rows // P):
                 q_codes[s, o, m0 // P + j] = codes[:, j * P : (j + 1) * P]
                 q_scales[s, o, m0 // P + j] = scales[:, j * P : (j + 1) * P]
@@ -93,7 +92,7 @@ def tile_attend_quest_topk_kernel(tc, qT, k_words, k_scales, c_words, c_scales, 
         words16 = {}
 
         def gather_words(s):
-            got = [reuse.tile([P, HALF], U32, name="got_words%d_%d" % (s, h), offset=((1024, 0), (1536, 2560))[s][h], align_bytes=64) for h in range(2)]
+            got = [reuse.tile([P, HALF], U32, name="got_words%d_%d" % (s, h), offset=((0, 1024), (1536, 2560))[s][h], align_bytes=64) for h in range(2)]
             for h in range(2):
                 lists = offsets[:, h * (HALF // 16) : (h + 1) * (HALF // 16)]
                 nc.vector.tensor_copy(got[h][:], word_win[s][:].bitcast(U32).indirect(lists))
@@ -137,14 +136,14 @@ def tile_attend_quest_topk_kernel(tc, qT, k_words, k_scales, c_words, c_scales, 
         nc.scalar.activation(lo0[:], flipped[:], mybir.ActivationFunctionType.Copy, scale=-1.0)
         quantise(0, 0, 0, NQ, hi0, keep.tile([P, NQ], U32, name="codes0_0", align_bytes=64))
         got = gather_words(0)
-        warm = psum.tile([P, HALF], F32, name="warm", tag="bank0_0")
-        for j in range(3):
+        warm = psum.tile([P, N], F32, name="warm", tag="bank0_0")
+        for m in range(2):
             nc.tensor.matmul_mx(
                 out=warm[:],
-                lhsT=q_codes[0, 0, 0].bitcast(FP8X4),
-                lhsT_scale=q_scales[0, 0, 0],
-                rhs=got[1][:].bitcast(U16)[:, (j % 2) * HALF : (j % 2 + 1) * HALF].bitcast(FP4X4),
-                rhs_scale=scale_tiles[0, 0, 0][:],
+                lhsT=q_codes[0, 0, m].bitcast(FP8X4),
+                lhsT_scale=q_scales[0, 0, m],
+                rhs=got[0][:].bitcast(U16).bitcast(FP4X4),
+                rhs_scale=q_codes[0, 0, m].bitcast(U8),
                 start=True,
                 stop=True,
             )

@@ -92,7 +92,7 @@ def tile_attend_quest_topk_kernel(tc, qT, k_words, k_scales, c_words, c_scales, 
         words16 = {}
 
         def gather_words(s):
-            got = [reuse.tile([P, HALF], U32, name="got_words%d_%d" % (s, h), offset=((0, 1024), (1536, 2560))[s][h], align_bytes=64) for h in range(2)]
+            got = [reuse.tile([P, HALF], U32, name="got_words%d_%d" % (s, h), offset=((1024, 0), (1536, 2560))[s][h], align_bytes=64) for h in range(2)]
             for h in range(2):
                 lists = offsets[:, h * (HALF // 16) : (h + 1) * (HALF // 16)]
                 nc.vector.tensor_copy(got[h][:], word_win[s][:].bitcast(U32).indirect(lists))
@@ -142,7 +142,7 @@ def tile_attend_quest_topk_kernel(tc, qT, k_words, k_scales, c_words, c_scales, 
                 out=warm[:],
                 lhsT=q_codes[0, 0, m].bitcast(FP8X4),
                 lhsT_scale=q_scales[0, 0, m],
-                rhs=got[0][:].bitcast(U16).bitcast(FP4X4),
+                rhs=got[1][:].bitcast(U16).bitcast(FP4X4),
                 rhs_scale=q_codes[0, 0, m].bitcast(U8),
                 start=True,
                 stop=True,

@@ -14,189 +14,179 @@ U8 = mybir.dt.uint8
 FP8X4 = mybir.dt.float8_e4m3fn_x4
 FP4X4 = mybir.dt.float4_e2m1fn_x4
 RELU = mybir.ActivationFunctionType.Relu
+COPY = mybir.ActivationFunctionType.Copy
 
 P = 128
 PACK = 4
 PASSES = 2
-HALF = N // 2
-NB = 128
+K, C = 0, 1
+BLOCKS = ((0, 128), (128, 256), (384, 128))
 
 
 def tile_attend_quest_topk_kernel(tc, qT, k_words, k_scales, c_words, c_scales, offs, out):
     nc = tc.nc
     with ExitStack() as ctx:
         keep = ctx.enter_context(tc.tile_pool(name="keep", bufs=1))
-        late = ctx.enter_context(tc.tile_pool(name="late", bufs=1))
         reuse = ctx.enter_context(tc.tile_pool(name="reuse", bufs=1))
         psum = ctx.enter_context(tc.psum_pool(name="psum", bufs=1))
+
+        def kept(name, width, dtype, tag=None):
+            return keep.tile([P, width], dtype, name=name, tag=tag or name, align_bytes=64)
+
+        def laid(name, width, dtype, offset):
+            return reuse.tile([P, width], dtype, name=name, offset=offset, align_bytes=64)
 
         offsets = keep.tile([P, N // 16], U16, name="offsets")
         nc.sync.dma_start(offsets[:], offs)
 
         scale_win = []
         for name, scales in (("k", k_scales), ("c", c_scales)):
-            win = keep.tile([P, T], U8, name=name + "_scale_win", tag=name + "_stage", align_bytes=64)
-            nc.scalar.dma_start(win[96:128, :].bitcast(I32), scales.bitcast(I32).rearrange("o f w -> f o w"))
+            win = laid(name + "_scale_win", T, U8, 12288) if name == "k" else kept(name + "_scale_win", T, U8)
+            (nc.scalar if name == "k" else nc.sync).dma_start(win[96:128, :].bitcast(I32), scales.bitcast(I32).rearrange("o f w -> f o w"))
             nc.vector.memset(win[0:96, :].bitcast(I32), 0)
             scale_win.append(win)
-        planes = keep.tile([P, PASSES * 2 * N], U8, name="planes", align_bytes=64)
-        nc.vector.memset(planes[:].bitcast(I32), 0)
+        planes = [kept("planes%d" % s, PASSES * N, U8) for s in (K, C)]
+        for s in (K, C):
+            nc.vector.memset(planes[s][:].bitcast(I32), 0)
 
-        def load_q(o, queue, tag):
-            raw = keep.tile([P, PACK, NQ], F32, name="q_raw%d" % o, tag=tag, align_bytes=64)
-            queue.dma_start(raw[:], qT[0, 512 * o : 512 * (o + 1), :].rearrange("(p t) m -> p t m", t=PACK))
-            return raw
+        q_rows = [qT[0, 512 * o : 512 * (o + 1), :].rearrange("(p t) m -> p (t m)", t=PACK) for o in range(PASSES)]
+        q_flat0 = kept("q_raw0", PACK * NQ, F32)
+        nc.scalar.dma_start(q_flat0[:], q_rows[0])
+        word_win = [laid("k_word_win", T, I32, 20480), laid("c_word_win", T, I32, 12288)]
+        word_rows = [words[0].rearrange("p t b -> p (t b)").bitcast(I32) for words in (k_words, c_words)]
+        nc.scalar.dma_start(word_win[K][:], word_rows[K])
+        q_flat1 = kept("q_raw1", PACK * NQ, F32)
+        nc.scalar.dma_start(q_flat1[:], q_rows[1])
 
-        q_raw0 = load_q(0, nc.scalar, "q_stage")
-        word_win = []
-        word_win.append(keep.tile([P, T], I32, name="k_word_win", align_bytes=64))
-        word_win.append(late.tile([P, T], I32, name="c_word_win", offset=0, align_bytes=64))
-        for win, words in zip(word_win, (k_words, c_words)):
-            nc.scalar.dma_start(win[:], words[0].rearrange("p t b -> p (t b)").bitcast(I32))
+        def lay_planes(s):
+            got = kept("got_scales%d" % s, N, U8)
+            nc.vector.tensor_copy(got[:], scale_win[s][:].indirect(offsets[:]))
+            for quad in range(4):
+                nc.sync.dma_start(
+                    planes[s][32 * quad : 32 * quad + 4, :].bitcast(I32).rearrange("p (o w) -> p o w", o=PASSES),
+                    got[96 + 8 * quad : 96 + 8 * quad + 8, :].bitcast(I32),
+                )
 
-        got_scales = keep.tile([P, 2 * N], U8, name="got_scales", align_bytes=64)
-        for s in range(2):
-            nc.vector.tensor_copy(got_scales[:, s * N : (s + 1) * N], scale_win[s][:].indirect(offsets[:]))
-        for quad in range(4):
-            nc.sync.dma_start(
-                planes[32 * quad : 32 * quad + 4, :].bitcast(I32).rearrange("p (o w) -> p o w", o=PASSES),
-                got_scales[96 + 8 * quad : 96 + 8 * quad + 8, :].bitcast(I32),
-            )
-        q_rows1 = qT[0, 512:1024, :].rearrange("(p t) m -> p (t m)", t=PACK)
-        q_flat1 = keep.tile([P, PACK * NQ], F32, name="q_raw1", tag="c_stage", align_bytes=64)
-        for u in range(2):
-            nc.sync.dma_start(q_flat1[:, 2 * u * NQ : 2 * (u + 1) * NQ], q_rows1[:, 2 * u * NQ : 2 * (u + 1) * NQ])
-        q_raw1 = q_flat1[:].rearrange("p (t m) -> p t m", t=PACK)
+        lay_planes(K)
+        nc.sync.dma_start(word_win[C][:], word_rows[C])
+        lay_planes(C)
+        q_raw = [flat[:].rearrange("p (t m) -> p t m", t=PACK) for flat in (q_flat0, q_flat1)]
+
+        def views(o, m0, rows, part):
+            src = q_raw[o][:, :, m0 : m0 + rows].rearrange("p t (c i) -> p c t i", i=4)
+            return part.rearrange("p (c i t) -> p c t i", i=4, t=PACK), src
 
         q_codes, q_scales = {}, {}
 
-        def views(raw, m0, rows, part):
-            src = raw[:, :, m0 : m0 + rows].rearrange("p t (c i) -> p c t i", i=4)
-            return part[:].rearrange("p (c i t) -> p c t i", i=4, t=PACK), src
-
-        def positive_part(raw, m0, rows, part):
-            dst, src = views(raw, m0, rows, part)
-            nc.scalar.activation(dst, src, RELU)
-
-        def negative_part(raw, m0, rows, part):
-            dst, src = views(raw, m0, rows, part)
-            nc.vector.tensor_scalar_min(dst, src, 0.0)
-
         def quantise(s, o, m0, rows, part, codes):
-            scales = keep.tile([P, rows], U8, name="q_scales%d_%d_%d" % (s, o, m0), align_bytes=64)
+            scales = kept("q_scales%d_%d_%d" % (s, o, m0), rows, U8)
             nc.vector.quantize_mx(out=codes[:].bitcast(FP8X4), scales=scales[:], in_=part[:])
             for j in range(rows // P):
                 q_codes[s, o, m0 // P + j] = codes[:, j * P : (j + 1) * P]
                 q_scales[s, o, m0 // P + j] = scales[:, j * P : (j + 1) * P]
 
+        def gather(s, got, n0, width):
+            lists = offsets[:, n0 // 16 : (n0 + width) // 16]
+            nc.vector.tensor_copy(got[:], word_win[s][:].bitcast(U32).indirect(lists))
+
         words16 = {}
 
-        def gather_words(s):
-            got = [reuse.tile([P, HALF], U32, name="got_words%d_%d" % (s, h), offset=((1024, 0), (1536, 2560))[s][h], align_bytes=64) for h in range(2)]
-            for h in range(2):
-                lists = offsets[:, h * (HALF // 16) : (h + 1) * (HALF // 16)]
-                nc.vector.tensor_copy(got[h][:], word_win[s][:].bitcast(U32).indirect(lists))
-            return got
-
-        def part_words(s, got, b0, blocks):
-            width = blocks * NB
-            parted = keep.tile([P, PASSES * width], U16, name="words16_%d_%d" % (s, b0), align_bytes=64)
-            c0 = (b0 % 2) * NB
+        def part_words(s, got, parted, blocks):
+            width = sum(BLOCKS[b][1] for b in blocks)
             nc.vector.tensor_copy(
                 parted[:].rearrange("p (o n) -> p o n", o=PASSES),
-                got[b0 // 2][:, c0 : c0 + width].bitcast(U16).rearrange("p (n o) -> p o n", o=PASSES),
+                got[:].bitcast(U16).rearrange("p (n o) -> p o n", o=PASSES),
             )
             for o in range(PASSES):
-                for j in range(blocks):
-                    words16[s, o, b0 + j] = parted[:, o * width + j * NB : o * width + (j + 1) * NB]
-            return parted
+                for b in blocks:
+                    c0 = o * width + BLOCKS[b][0] - BLOCKS[blocks[0]][0]
+                    words16[s, o, b] = parted[:, c0 : c0 + BLOCKS[b][1]]
 
-        banks = {}
+        banks = {
+            (m, b): psum.tile([P, BLOCKS[b][1]], F32, name="bank%d_%d" % (m, b), tag="bank%d_%d" % (m, b))
+            for m in range(2)
+            for b in range(3)
+        }
 
         def multiply(s, o, m, b):
-            if (m, b) not in banks:
-                banks.setdefault((m, b), psum.tile([P, NB], F32, name="bank%d_%d" % (m, b), tag="bank%d_%d" % (m, b)))
-            plane0 = (o * 2 + s) * N + b * NB
+            n0, width = BLOCKS[b]
+            plane0 = o * N + n0
             nc.tensor.matmul_mx(
                 out=banks[m, b][:],
                 lhsT=q_codes[s, o, m].bitcast(FP8X4),
                 lhsT_scale=q_scales[s, o, m],
                 rhs=words16[s, o, b].bitcast(FP4X4),
-                rhs_scale=planes[:, plane0 : plane0 + NB],
-                start=(s == 0 and o == 0),
-                stop=(s == 1 and o == PASSES - 1),
+                rhs_scale=planes[s][:, plane0 : plane0 + width],
+                start=(s == K and o == 0),
+                stop=(s == C and o == PASSES - 1),
             )
 
-        hi0 = reuse.tile([P, NQ * PACK], BF16, name="hi0", offset=0, align_bytes=64)
-        lo0 = reuse.tile([P, NQ * PACK], BF16, name="lo0", offset=2048, align_bytes=64)
-        positive_part(q_raw0, 0, NQ, hi0)
-        flipped = reuse.tile([P, NQ * PACK], BF16, name="flipped", offset=4096, align_bytes=64)
-        dst, src = views(q_raw0, 0, NQ, flipped)
+        hi0 = laid("hi0", NQ * PACK, BF16, 0)
+        lo0 = [kept("lo0_%d" % m, P * PACK, BF16) for m in range(2)]
+        flipped = laid("flipped", P * PACK, BF16, 8192)
+        dst, src = views(0, 0, NQ, hi0[:])
+        nc.scalar.activation(dst, src, RELU)
+        dst, src = views(0, P, P, flipped[:])
         nc.scalar.activation(dst, src, RELU, scale=-1.0)
-        nc.scalar.activation(lo0[:], flipped[:], mybir.ActivationFunctionType.Copy, scale=-1.0)
-        quantise(0, 0, 0, NQ, hi0, keep.tile([P, NQ], U32, name="codes0_0", align_bytes=64))
-        got = gather_words(0)
-        warm = psum.tile([P, N], F32, name="warm", tag="bank0_0")
-        for m in range(2):
-            nc.tensor.matmul_mx(
-                out=warm[:],
-                lhsT=q_codes[0, 0, m].bitcast(FP8X4),
-                lhsT_scale=q_scales[0, 0, m],
-                rhs=got[1][:].bitcast(U16).bitcast(FP4X4),
-                rhs_scale=q_codes[0, 0, m].bitcast(U8),
-                start=True,
-                stop=True,
-            )
-        part_words(0, got, 0, 2)
-        quantise(1, 0, 0, NQ, lo0, keep.tile([P, NQ], U32, name="codes0_1", align_bytes=64))
-        part_words(0, got, 2, 2)
-        for b in range(N // NB):
-            for m in range(2):
-                multiply(0, 0, m, b)
-        got = gather_words(1)
-        for b0, blocks in [[0,2],[2,2]]:
-            part_words(1, got, b0, blocks)
-            for b in range(b0, b0 + blocks):
+        nc.scalar.activation(lo0[1][:], flipped[:], COPY, scale=-1.0)
+        dst, src = views(0, 0, P, lo0[0][:])
+        nc.vector.tensor_scalar_min(dst, src, 0.0)
+        quantise(K, 0, 0, NQ, hi0, kept("codes_hi0", NQ, U32))
+        quantise(C, 0, 0, P, lo0[0], kept("codes_lo0_0", P, U32))
+        got_k = [laid("got_k0", 384, U32, 512), laid("got_k1", 128, U32, 0)]
+        gather(K, got_k[0], 0, 384)
+        gather(K, got_k[1], 384, 128)
+        part_words(K, got_k[0], kept("parted_k0", 768, U16), [0, 1])
+        part_words(K, got_k[1], kept("parted_k1", 256, U16), [2])
+        hi1 = laid("hi1", NQ * PACK, BF16, 8192)
+        lo1 = laid("lo1", NQ * PACK, BF16, 20480)
+        dst, src = views(1, 0, NQ, hi1[:])
+        nc.scalar.activation(dst, src, RELU)
+        dst, src = views(1, 0, NQ, lo1[:])
+        nc.vector.tensor_scalar_min(dst, src, 0.0)
+        quantise(C, 0, P, P, lo0[1], laid("codes_lo0_1", P, U32, 24576))
+        quantise(K, 1, 0, NQ, hi1, kept("codes_hi1", NQ, U32))
+        quantise(C, 1, 0, NQ, lo1, kept("codes_lo1", NQ, U32))
+        for o in range(PASSES):
+            for b in range(3):
                 for m in range(2):
-                    multiply(1, 0, m, b)
+                    multiply(K, o, m, b)
 
-        hi1 = [reuse.tile([P, P * PACK], BF16, name="hi1_%d" % m, offset=4096 + 1024 * m, align_bytes=64) for m in range(2)]
-        lo1 = [late.tile([P, P * PACK], BF16, name="lo1_%d" % m, offset=2048 * m, align_bytes=64) for m in range(2)]
-        codes1 = {
-            (s, m): late.tile([P, P], U32, name="codes1_%d_%d" % (s, m), offset=2048 * m + 1024 + 512 * s, align_bytes=64)
-            for s in range(2)
-            for m in range(2)
-        }
-        dst, src = views(q_raw1, 0, P, hi1[0])
-        for u in range(2):
-            nc.scalar.activation(dst[:, :, 2 * u : 2 * u + 2, :], src[:, :, 2 * u : 2 * u + 2, :], RELU)
-        positive_part(q_raw1, P, P, hi1[1])
+        got_c = [laid("got_c0", 128, U32, 8192), laid("got_c1", 256, U32, 9216), laid("got_c2", 128, U32, 8192)]
+        out_by_tile = out[0].rearrange("(m p) n -> p m n", p=P)
 
-        def products(s, m):
-            for b in range(N // NB):
-                multiply(s, 1, m, b)
+        def products(b):
+            part_words(C, got_c[b], kept("parted_c%d" % b, 2 * BLOCKS[b][1], U16), [b])
+            for m in range(2):
+                for o in range(PASSES):
+                    multiply(C, o, m, b)
 
-        copiers = {"S": nc.scalar.copy, "V": nc.vector.tensor_copy}
-        queues = {"sync": nc.sync, "scalar": nc.scalar}
+        def leave_tile(b, m, copy):
+            n0, width = BLOCKS[b]
+            staged = kept("staged%d_%d" % (b, m), width, F32)
+            copy(staged[:], banks[m, b][:])
+            nc.sync.dma_start(out[0, m * P : (m + 1) * P, n0 : n0 + width], staged[:])
 
-        def leave(m):
-            for mm, b0, blocks, queue in [[0,0,2,"sync"],[0,2,2,"sync"],[1,0,2,"sync"],[1,2,2,"sync"]]:
-                if mm == m:
-                    staged = keep.tile([P, blocks * NB], F32, name="staged%d_%d" % (m, b0), align_bytes=64)
-                    for j in range(blocks):
-                        copiers[["SSSS","SVSV"][m][b0 + j]](staged[:, j * NB : (j + 1) * NB], banks[m, b0 + j][:])
-                    queues[queue].dma_start(out[0, m * P : (m + 1) * P, b0 * NB : (b0 + blocks) * NB], staged[:])
+        def leave_both(b, copies):
+            n0, width = BLOCKS[b]
+            staged = kept("staged%d" % b, 2 * width, F32)
+            for m in range(2):
+                copies[m](staged[:, m * width : (m + 1) * width], banks[m, b][:])
+            nc.sync.dma_start(out_by_tile[:, :, n0 : n0 + width], staged[:].rearrange("p (m n) -> p m n", m=2))
 
-        negative_part(q_raw1, 0, P, lo1[0])
-        quantise(0, 1, 0, P, hi1[0], codes1[0, 0])
-        products(0, 0)
-        negative_part(q_raw1, P, P // 2, lo1[1][:, 0 : P * PACK // 2])
-        quantise(1, 1, 0, P, lo1[0], codes1[1, 0])
-        products(1, 0)
-        leave(0)
-        negative_part(q_raw1, P + P // 2, P // 2, lo1[1][:, P * PACK // 2 : P * PACK])
-        quantise(0, 1, P, P, hi1[1], codes1[0, 1])
-        products(0, 1)
-        quantise(1, 1, P, P, lo1[1], codes1[1, 1])
-        products(1, 1)
-        leave(1)
+        gather(C, got_c[0], *BLOCKS[0])
+        gather(C, got_c[1], *BLOCKS[1])
+        products(0)
+        products(1)
+        gather(C, got_c[2], *BLOCKS[2])
+        halves = got_c[2][:].bitcast(U16).rearrange("p (n o) -> p o n", o=PASSES)
+        for o in range(PASSES):
+            parted = kept("parted_c2_%d" % o, BLOCKS[2][1], U16)
+            nc.vector.tensor_copy(parted[:], halves[:, o, :])
+            words16[C, o, 2] = parted[:]
+            for m in range(2):
+                multiply(C, o, m, 2)
+        leave_both(0, (nc.scalar.copy, nc.scalar.copy))
+        leave_tile(1, 0, nc.scalar.copy)
+        leave_tile(1, 1, nc.vector.tensor_copy)
+        leave_both(2, (nc.vector.tensor_copy, nc.scalar.copy))

@@ -42,7 +42,7 @@ def tile_attend_quest_topk_kernel(tc, qT, k_words, k_scales, c_words, c_scales, 
         scale_win = []
         for name, scales in (("k", k_scales), ("c", c_scales)):
             win = laid(name + "_scale_win", T, U8, 12288) if name == "k" else kept(name + "_scale_win", T, U8)
-            (nc.scalar if name == "k" else nc.sync).dma_start(win[96:128, :].bitcast(I32), scales.bitcast(I32).rearrange("o f w -> f o w"))
+            nc.sync.dma_start(win[96:128, :].bitcast(I32), scales.bitcast(I32).rearrange("o f w -> f o w"))
             nc.vector.memset(win[0:96, :].bitcast(I32), 0)
             scale_win.append(win)
         planes = [kept("planes%d" % s, PASSES * N, U8) for s in (K, C)]
@@ -51,12 +51,12 @@ def tile_attend_quest_topk_kernel(tc, qT, k_words, k_scales, c_words, c_scales, 
 
         q_rows = [qT[0, 512 * o : 512 * (o + 1), :].rearrange("(p t) m -> p (t m)", t=PACK) for o in range(PASSES)]
         q_flat0 = kept("q_raw0", PACK * NQ, F32)
-        nc.scalar.dma_start(q_flat0[:], q_rows[0])
+        nc.sync.dma_start(q_flat0[:], q_rows[0])
         word_win = [laid("k_word_win", T, I32, 20480), laid("c_word_win", T, I32, 12288)]
         word_rows = [words[0].rearrange("p t b -> p (t b)").bitcast(I32) for words in (k_words, c_words)]
-        nc.scalar.dma_start(word_win[K][:], word_rows[K])
+        nc.sync.dma_start(word_win[K][:], word_rows[K])
         q_flat1 = kept("q_raw1", PACK * NQ, F32)
-        nc.scalar.dma_start(q_flat1[:], q_rows[1])
+        nc.sync.dma_start(q_flat1[:], q_rows[1])
 
         def lay_planes(s):
             got = kept("got_scales%d" % s, N, U8)

@@ -14,7 +14,6 @@ U8 = mybir.dt.uint8
 FP8X4 = mybir.dt.float8_e4m3fn_x4
 FP4X4 = mybir.dt.float4_e2m1fn_x4
 RELU = mybir.ActivationFunctionType.Relu
-COPY = mybir.ActivationFunctionType.Copy
 
 P = 128
 PACK = 4
@@ -42,7 +41,7 @@ def tile_attend_quest_topk_kernel(tc, qT, k_words, k_scales, c_words, c_scales, 
         scale_win = []
         for name, scales in (("k", k_scales), ("c", c_scales)):
             win = laid(name + "_scale_win", T, U8, 12288) if name == "k" else kept(name + "_scale_win", T, U8)
-            nc.sync.dma_start(win[96:128, :].bitcast(I32), scales.bitcast(I32).rearrange("o f w -> f o w"))
+            (nc.scalar if name == "k" else nc.sync).dma_start(win[96:128, :].bitcast(I32), scales.bitcast(I32).rearrange("o f w -> f o w"))
             nc.vector.memset(win[0:96, :].bitcast(I32), 0)
             scale_win.append(win)
         planes = [kept("planes%d" % s, PASSES * N, U8) for s in (K, C)]
@@ -51,12 +50,12 @@ def tile_attend_quest_topk_kernel(tc, qT, k_words, k_scales, c_words, c_scales, 
 
         q_rows = [qT[0, 512 * o : 512 * (o + 1), :].rearrange("(p t) m -> p (t m)", t=PACK) for o in range(PASSES)]
         q_flat0 = kept("q_raw0", PACK * NQ, F32)
-        nc.sync.dma_start(q_flat0[:], q_rows[0])
+        nc.scalar.dma_start(q_flat0[:], q_rows[0])
         word_win = [laid("k_word_win", T, I32, 20480), laid("c_word_win", T, I32, 12288)]
         word_rows = [words[0].rearrange("p t b -> p (t b)").bitcast(I32) for words in (k_words, c_words)]
-        nc.sync.dma_start(word_win[K][:], word_rows[K])
+        nc.scalar.dma_start(word_win[K][:], word_rows[K])
         q_flat1 = kept("q_raw1", PACK * NQ, F32)
-        nc.sync.dma_start(q_flat1[:], q_rows[1])
+        nc.scalar.dma_start(q_flat1[:], q_rows[1])
 
         def lay_planes(s):
             got = kept("got_scales%d" % s, N, U8)
@@ -122,17 +121,13 @@ def tile_attend_quest_topk_kernel(tc, qT, k_words, k_scales, c_words, c_scales, 
             )
 
         hi0 = laid("hi0", NQ * PACK, BF16, 0)
-        lo0 = [kept("lo0_%d" % m, P * PACK, BF16) for m in range(2)]
-        flipped = laid("flipped", P * PACK, BF16, 8192)
+        lo0 = kept("lo0", NQ * PACK, BF16)
         dst, src = views(0, 0, NQ, hi0[:])
         nc.scalar.activation(dst, src, RELU)
-        dst, src = views(0, P, P, flipped[:])
-        nc.scalar.activation(dst, src, RELU, scale=-1.0)
-        nc.scalar.activation(lo0[1][:], flipped[:], COPY, scale=-1.0)
-        dst, src = views(0, 0, P, lo0[0][:])
+        dst, src = views(0, 0, NQ, lo0[:])
         nc.vector.tensor_scalar_min(dst, src, 0.0)
         quantise(K, 0, 0, NQ, hi0, kept("codes_hi0", NQ, U32))
-        quantise(C, 0, 0, P, lo0[0], kept("codes_lo0_0", P, U32))
+        quantise(C, 0, 0, NQ, lo0, kept("codes_lo0", NQ, U32))
         got_k = [laid("got_k0", 384, U32, 512), laid("got_k1", 128, U32, 0)]
         gather(K, got_k[0], 0, 384)
         gather(K, got_k[1], 384, 128)
@@ -144,7 +139,6 @@ def tile_attend_quest_topk_kernel(tc, qT, k_words, k_scales, c_words, c_scales, 
         nc.scalar.activation(dst, src, RELU)
         dst, src = views(1, 0, NQ, lo1[:])
         nc.vector.tensor_scalar_min(dst, src, 0.0)
-        quantise(C, 0, P, P, lo0[1], laid("codes_lo0_1", P, U32, 24576))
         quantise(K, 1, 0, NQ, hi1, kept("codes_hi1", NQ, U32))
         quantise(C, 1, 0, NQ, lo1, kept("codes_lo1", NQ, U32))
         for o in range(PASSES):

@@ -18,8 +18,14 @@ RELU = mybir.ActivationFunctionType.Relu
 P = 128
 PACK = 4
 PASSES = 2
+TILES = NQ // P
 K, C = 0, 1
 BLOCKS = ((0, 128), (128, 256), (384, 128))
+
+AT_HI0 = 0
+AT_HI1 = 8192
+AT_K_SCALES = 12288
+AT_K_WORDS = 20480
 
 
 def tile_attend_quest_topk_kernel(tc, qT, k_words, k_scales, c_words, c_scales, offs, out):
@@ -29,8 +35,8 @@ def tile_attend_quest_topk_kernel(tc, qT, k_words, k_scales, c_words, c_scales, 
         reuse = ctx.enter_context(tc.tile_pool(name="reuse", bufs=1))
         psum = ctx.enter_context(tc.psum_pool(name="psum", bufs=1))
 
-        def kept(name, width, dtype, tag=None):
-            return keep.tile([P, width], dtype, name=name, tag=tag or name, align_bytes=64)
+        def kept(name, width, dtype):
+            return keep.tile([P, width], dtype, name=name, tag=name, align_bytes=64)
 
         def laid(name, width, dtype, offset):
             return reuse.tile([P, width], dtype, name=name, offset=offset, align_bytes=64)
@@ -38,24 +44,22 @@ def tile_attend_quest_topk_kernel(tc, qT, k_words, k_scales, c_words, c_scales, 
         offsets = keep.tile([P, N // 16], U16, name="offsets")
         nc.sync.dma_start(offsets[:], offs)
 
-        scale_win = []
-        for name, scales in (("k", k_scales), ("c", c_scales)):
-            win = laid(name + "_scale_win", T, U8, 12288) if name == "k" else kept(name + "_scale_win", T, U8)
-            (nc.scalar if name == "k" else nc.sync).dma_start(win[96:128, :].bitcast(I32), scales.bitcast(I32).rearrange("o f w -> f o w"))
+        scale_win = [laid("k_scale_win", T, U8, AT_K_SCALES), kept("c_scale_win", T, U8)]
+        for win, scales, queue in ((scale_win[K], k_scales, nc.scalar), (scale_win[C], c_scales, nc.sync)):
+            queue.dma_start(win[96:128, :].bitcast(I32), scales.bitcast(I32).rearrange("o f w -> f o w"))
             nc.vector.memset(win[0:96, :].bitcast(I32), 0)
-            scale_win.append(win)
         planes = [kept("planes%d" % s, PASSES * N, U8) for s in (K, C)]
         for s in (K, C):
             nc.vector.memset(planes[s][:].bitcast(I32), 0)
 
-        q_rows = [qT[0, 512 * o : 512 * (o + 1), :].rearrange("(p t) m -> p (t m)", t=PACK) for o in range(PASSES)]
-        q_flat0 = kept("q_raw0", PACK * NQ, F32)
-        nc.scalar.dma_start(q_flat0[:], q_rows[0])
-        word_win = [laid("k_word_win", T, I32, 20480), laid("c_word_win", T, I32, 12288)]
-        word_rows = [words[0].rearrange("p t b -> p (t b)").bitcast(I32) for words in (k_words, c_words)]
-        nc.scalar.dma_start(word_win[K][:], word_rows[K])
-        q_flat1 = kept("q_raw1", PACK * NQ, F32)
-        nc.scalar.dma_start(q_flat1[:], q_rows[1])
+        q_raw = [kept("q_raw%d" % o, PACK * NQ, F32) for o in range(PASSES)]
+        word_win = [laid("k_word_win", T, I32, AT_K_WORDS), laid("c_word_win", T, I32, AT_K_SCALES)]
+
+        def load_q(o):
+            nc.scalar.dma_start(q_raw[o][:], qT[0, 512 * o : 512 * (o + 1), :].rearrange("(p t) m -> p (t m)", t=PACK))
+
+        def load_words(s, words, queue):
+            queue.dma_start(word_win[s][:], words[0].rearrange("p t b -> p (t b)").bitcast(I32))
 
         def lay_planes(s):
             got = kept("got_scales%d" % s, N, U8)
@@ -66,94 +70,114 @@ def tile_attend_quest_topk_kernel(tc, qT, k_words, k_scales, c_words, c_scales, 
                     got[96 + 8 * quad : 96 + 8 * quad + 8, :].bitcast(I32),
                 )
 
+        load_q(0)
+        load_words(K, k_words, nc.scalar)
+        load_q(1)
         lay_planes(K)
-        nc.sync.dma_start(word_win[C][:], word_rows[C])
+        load_words(C, c_words, nc.sync)
         lay_planes(C)
-        q_raw = [flat[:].rearrange("p (t m) -> p t m", t=PACK) for flat in (q_flat0, q_flat1)]
 
-        def views(o, m0, rows, part):
-            src = q_raw[o][:, :, m0 : m0 + rows].rearrange("p t (c i) -> p c t i", i=4)
-            return part.rearrange("p (c i t) -> p c t i", i=4, t=PACK), src
+        def interleaved(o, part):
+            src = q_raw[o][:].rearrange("p (t c i) -> p c t i", t=PACK, i=4)
+            return part[:].rearrange("p (c i t) -> p c t i", i=4, t=PACK), src
+
+        def positive(o, part):
+            dst, src = interleaved(o, part)
+            nc.scalar.activation(dst, src, RELU)
+
+        def negative(o, part):
+            dst, src = interleaved(o, part)
+            nc.vector.tensor_scalar_min(dst, src, 0.0)
 
         q_codes, q_scales = {}, {}
 
-        def quantise(s, o, m0, rows, part, codes):
-            scales = kept("q_scales%d_%d_%d" % (s, o, m0), rows, U8)
+        def quantise(s, o, part, codes):
+            scales = kept("q_scales%d_%d" % (s, o), NQ, U8)
             nc.vector.quantize_mx(out=codes[:].bitcast(FP8X4), scales=scales[:], in_=part[:])
-            for j in range(rows // P):
-                q_codes[s, o, m0 // P + j] = codes[:, j * P : (j + 1) * P]
-                q_scales[s, o, m0 // P + j] = scales[:, j * P : (j + 1) * P]
+            q_codes[s, o], q_scales[s, o] = codes, scales
 
-        def gather(s, got, n0, width):
+        def gather(s, b, at):
+            n0, width = BLOCKS[b]
+            got = laid("got%d_%d" % (s, b), width, U32, at)
             lists = offsets[:, n0 // 16 : (n0 + width) // 16]
             nc.vector.tensor_copy(got[:], word_win[s][:].bitcast(U32).indirect(lists))
+            return got
 
         words16 = {}
 
-        def part_words(s, got, parted, blocks):
-            width = sum(BLOCKS[b][1] for b in blocks)
+        def part_block(s, b, got):
+            width = BLOCKS[b][1]
+            parted = kept("parted%d_%d" % (s, b), PASSES * width, U16)
             nc.vector.tensor_copy(
                 parted[:].rearrange("p (o n) -> p o n", o=PASSES),
                 got[:].bitcast(U16).rearrange("p (n o) -> p o n", o=PASSES),
             )
             for o in range(PASSES):
-                for b in blocks:
-                    c0 = o * width + BLOCKS[b][0] - BLOCKS[blocks[0]][0]
-                    words16[s, o, b] = parted[:, c0 : c0 + BLOCKS[b][1]]
+                words16[s, o, b] = parted[:, o * width : (o + 1) * width]
+
+        def part_pass(s, b, o, got):
+            parted = kept("parted%d_%d_%d" % (s, b, o), BLOCKS[b][1], U16)
+            nc.vector.tensor_copy(parted[:], got[:].bitcast(U16).rearrange("p (n o) -> p o n", o=PASSES)[:, o, :])
+            words16[s, o, b] = parted[:]
 
         banks = {
             (m, b): psum.tile([P, BLOCKS[b][1]], F32, name="bank%d_%d" % (m, b), tag="bank%d_%d" % (m, b))
-            for m in range(2)
-            for b in range(3)
+            for m in range(TILES)
+            for b in range(len(BLOCKS))
         }
 
-        def multiply(s, o, m, b):
+        def multiply(s, o, b):
             n0, width = BLOCKS[b]
-            plane0 = o * N + n0
-            nc.tensor.matmul_mx(
-                out=banks[m, b][:],
-                lhsT=q_codes[s, o, m].bitcast(FP8X4),
-                lhsT_scale=q_scales[s, o, m],
-                rhs=words16[s, o, b].bitcast(FP4X4),
-                rhs_scale=planes[s][:, plane0 : plane0 + width],
-                start=(s == K and o == 0),
-                stop=(s == C and o == PASSES - 1),
-            )
+            for m in range(TILES):
+                nc.tensor.matmul_mx(
+                    out=banks[m, b][:],
+                    lhsT=q_codes[s, o][:, m * P : (m + 1) * P].bitcast(FP8X4),
+                    lhsT_scale=q_scales[s, o][:, m * P : (m + 1) * P],
+                    rhs=words16[s, o, b].bitcast(FP4X4),
+                    rhs_scale=planes[s][:, o * N + n0 : o * N + n0 + width],
+                    start=(s == K and o == 0),
+                    stop=(s == C and o == PASSES - 1),
+                )
 
-        hi0 = laid("hi0", NQ * PACK, BF16, 0)
+        hi0 = laid("hi0", NQ * PACK, BF16, AT_HI0)
         lo0 = kept("lo0", NQ * PACK, BF16)
-        dst, src = views(0, 0, NQ, hi0[:])
-        nc.scalar.activation(dst, src, RELU)
-        dst, src = views(0, 0, NQ, lo0[:])
-        nc.vector.tensor_scalar_min(dst, src, 0.0)
-        quantise(K, 0, 0, NQ, hi0, kept("codes_hi0", NQ, U32))
-        quantise(C, 0, 0, NQ, lo0, kept("codes_lo0", NQ, U32))
-        got_k = [laid("got_k0", 384, U32, 512), laid("got_k1", 128, U32, 0)]
-        gather(K, got_k[0], 0, 384)
-        gather(K, got_k[1], 384, 128)
-        part_words(K, got_k[0], kept("parted_k0", 768, U16), [0, 1])
-        part_words(K, got_k[1], kept("parted_k1", 256, U16), [2])
-        hi1 = laid("hi1", NQ * PACK, BF16, 8192)
-        lo1 = laid("lo1", NQ * PACK, BF16, 20480)
-        dst, src = views(1, 0, NQ, hi1[:])
-        nc.scalar.activation(dst, src, RELU)
-        dst, src = views(1, 0, NQ, lo1[:])
-        nc.vector.tensor_scalar_min(dst, src, 0.0)
-        quantise(K, 1, 0, NQ, hi1, kept("codes_hi1", NQ, U32))
-        quantise(C, 1, 0, NQ, lo1, kept("codes_lo1", NQ, U32))
+        positive(0, hi0)
+        negative(0, lo0)
+        quantise(K, 0, hi0, kept("codes_hi0", NQ, U32))
+
+        first = gather(K, 0, AT_HI0)
+        middle = gather(K, 1, AT_HI0 + 512)
+        part_block(K, 0, first)
+        multiply(K, 0, 0)
+        part_block(K, 1, middle)
+        multiply(K, 0, 1)
+        last = gather(K, 2, AT_HI0)
+        quantise(C, 0, lo0, laid("codes_lo0", NQ, U32, AT_HI0 + 512))
+        part_block(K, 2, last)
+        multiply(K, 0, 2)
+
+        lo1 = laid("lo1", NQ * PACK, BF16, AT_K_WORDS)
+        negative(1, lo1)
+
+        hi1 = laid("hi1", NQ * PACK, BF16, AT_HI1)
+        positive(1, hi1)
+        quantise(K, 1, hi1, laid("codes_hi1", NQ, U32, AT_K_WORDS + 2048))
+        quantise(C, 1, lo1, kept("codes_lo1", NQ, U32))
+        for b in range(len(BLOCKS)):
+            multiply(K, 1, b)
+
+        first = gather(C, 0, AT_HI1)
+        middle = gather(C, 1, AT_HI1 + 1024)
+        for b, got in ((0, first), (1, middle)):
+            part_block(C, b, got)
+            for o in range(PASSES):
+                multiply(C, o, b)
+        last = gather(C, 2, AT_HI1)
         for o in range(PASSES):
-            for b in range(3):
-                for m in range(2):
-                    multiply(K, o, m, b)
+            part_pass(C, 2, o, last)
+            multiply(C, o, 2)
 
-        got_c = [laid("got_c0", 128, U32, 8192), laid("got_c1", 256, U32, 9216), laid("got_c2", 128, U32, 8192)]
         out_by_tile = out[0].rearrange("(m p) n -> p m n", p=P)
-
-        def products(b):
-            part_words(C, got_c[b], kept("parted_c%d" % b, 2 * BLOCKS[b][1], U16), [b])
-            for m in range(2):
-                for o in range(PASSES):
-                    multiply(C, o, m, b)
 
         def leave_tile(b, m, copy):
             n0, width = BLOCKS[b]
@@ -163,23 +187,11 @@ def tile_attend_quest_topk_kernel(tc, qT, k_words, k_scales, c_words, c_scales, 
 
         def leave_both(b, copies):
             n0, width = BLOCKS[b]
-            staged = kept("staged%d" % b, 2 * width, F32)
-            for m in range(2):
+            staged = kept("staged%d" % b, TILES * width, F32)
+            for m in range(TILES):
                 copies[m](staged[:, m * width : (m + 1) * width], banks[m, b][:])
-            nc.sync.dma_start(out_by_tile[:, :, n0 : n0 + width], staged[:].rearrange("p (m n) -> p m n", m=2))
+            nc.sync.dma_start(out_by_tile[:, :, n0 : n0 + width], staged[:].rearrange("p (m n) -> p m n", m=TILES))
 
-        gather(C, got_c[0], *BLOCKS[0])
-        gather(C, got_c[1], *BLOCKS[1])
-        products(0)
-        products(1)
-        gather(C, got_c[2], *BLOCKS[2])
-        halves = got_c[2][:].bitcast(U16).rearrange("p (n o) -> p o n", o=PASSES)
-        for o in range(PASSES):
-            parted = kept("parted_c2_%d" % o, BLOCKS[2][1], U16)
-            nc.vector.tensor_copy(parted[:], halves[:, o, :])
-            words16[C, o, 2] = parted[:]
-            for m in range(2):
-                multiply(C, o, m, 2)
         leave_both(0, (nc.scalar.copy, nc.scalar.copy))
         leave_tile(1, 0, nc.scalar.copy)
         leave_tile(1, 1, nc.vector.tensor_copy)

@@ -109,8 +109,8 @@ def tile_attend_quest_topk_kernel(tc, qT, k_words, k_scales, c_words, c_scales, 
             width = BLOCKS[b][1]
             parted = kept("parted%d_%d" % (s, b), PASSES * width, U16)
             nc.vector.tensor_copy(
-                parted[:].rearrange("p (o n) -> p o n", o=PASSES),
-                got[:].bitcast(U16).rearrange("p (n o) -> p o n", o=PASSES),
+                parted[:].rearrange("p (o h n) -> p h o n", o=PASSES, h=2),
+                got[:].bitcast(U16).rearrange("p (h n o) -> p h o n", o=PASSES, h=2),
             )
             for o in range(PASSES):
                 words16[s, o, b] = parted[:, o * width : (o + 1) * width]

@@ -20,9 +20,11 @@ PACK = 4
 PASSES = 2
 TILES = NQ // P
 K, C = 0, 1
+SCALE_ROW0 = (96, 32)
+SCALE_ZEROS = (((0, 96),), ((0, 32), (64, 128)))
 BLOCKS = ((0, 128), (128, 256), (384, 128))
 
-AT_HI0 = 0
+AT_LO0 = 0
 AT_HI1 = 8192
 AT_K_SCALES = 12288
 AT_K_WORDS = 20480
@@ -45,9 +47,11 @@ def tile_attend_quest_topk_kernel(tc, qT, k_words, k_scales, c_words, c_scales, 
         nc.sync.dma_start(offsets[:], offs)
 
         scale_win = [laid("k_scale_win", T, U8, AT_K_SCALES), kept("c_scale_win", T, U8)]
-        for win, scales, queue in ((scale_win[K], k_scales, nc.scalar), (scale_win[C], c_scales, nc.sync)):
-            queue.dma_start(win[96:128, :].bitcast(I32), scales.bitcast(I32).rearrange("o f w -> f o w"))
-            nc.vector.memset(win[0:96, :].bitcast(I32), 0)
+        for s, scales, queue in ((K, k_scales, nc.scalar), (C, c_scales, nc.sync)):
+            row0 = SCALE_ROW0[s]
+            queue.dma_start(scale_win[s][row0 : row0 + 32, :].bitcast(I32), scales.bitcast(I32).rearrange("o f w -> f o w"))
+            for lo, hi in SCALE_ZEROS[s]:
+                nc.vector.memset(scale_win[s][lo:hi, :].bitcast(I32), 0)
         planes = [kept("planes%d" % s, PASSES * N, U8) for s in (K, C)]
         for s in (K, C):
             nc.vector.memset(planes[s][:].bitcast(I32), 0)
@@ -61,21 +65,36 @@ def tile_attend_quest_topk_kernel(tc, qT, k_words, k_scales, c_words, c_scales, 
         def load_words(s, words, queue):
             queue.dma_start(word_win[s][:], words[0].rearrange("p t b -> p (t b)").bitcast(I32))
 
-        def lay_planes(s):
+        def gather_scales(s):
             got = kept("got_scales%d" % s, N, U8)
             nc.vector.tensor_copy(got[:], scale_win[s][:].indirect(offsets[:]))
-            for quad in range(4):
-                nc.sync.dma_start(
-                    planes[s][32 * quad : 32 * quad + 4, :].bitcast(I32).rearrange("p (o w) -> p o w", o=PASSES),
-                    got[96 + 8 * quad : 96 + 8 * quad + 8, :].bitcast(I32),
-                )
+            return got
+
+        def move_both(s, got, quad):
+            nc.sync.dma_start(
+                planes[s][32 * quad : 32 * quad + 4, :].bitcast(I32).rearrange("p (o w) -> p o w", o=PASSES),
+                got[SCALE_ROW0[s] + 8 * quad : SCALE_ROW0[s] + 8 * quad + 8, :].bitcast(I32),
+            )
+
+        def move_pass(s, got, quad, o):
+            nc.sync.dma_start(
+                planes[s][32 * quad : 32 * quad + 4, o * N : (o + 1) * N].bitcast(I32),
+                got[SCALE_ROW0[s] + 8 * quad + o : SCALE_ROW0[s] + 8 * quad + 8 : 2, :].bitcast(I32),
+            )
 
         load_q(0)
         load_words(K, k_words, nc.scalar)
         load_q(1)
-        lay_planes(K)
+        got = gather_scales(K)
+        for quad in range(3):
+            move_pass(K, got, quad, 0)
+        move_both(K, got, 3)
         load_words(C, c_words, nc.sync)
-        lay_planes(C)
+        for quad in range(3):
+            move_pass(K, got, quad, 1)
+        got = gather_scales(C)
+        for quad in range(4):
+            move_both(C, got, quad)
 
         def interleaved(o, part):
             src = q_raw[o][:].rearrange("p (t c i) -> p c t i", t=PACK, i=4)
@@ -96,9 +115,8 @@ def tile_attend_quest_topk_kernel(tc, qT, k_words, k_scales, c_words, c_scales, 
             nc.vector.quantize_mx(out=codes[:].bitcast(FP8X4), scales=scales[:], in_=part[:])
             q_codes[s, o], q_scales[s, o] = codes, scales
 
-        def gather(s, b, at):
-            n0, width = BLOCKS[b]
-            got = laid("got%d_%d" % (s, b), width, U32, at)
+        def gather(s, n0, width, at):
+            got = laid("got%d_%d" % (s, n0), width, U32, at)
             lists = offsets[:, n0 // 16 : (n0 + width) // 16]
             nc.vector.tensor_copy(got[:], word_win[s][:].bitcast(U32).indirect(lists))
             return got
@@ -139,22 +157,36 @@ def tile_attend_quest_topk_kernel(tc, qT, k_words, k_scales, c_words, c_scales, 
                     stop=(s == C and o == PASSES - 1),
                 )
 
-        hi0 = laid("hi0", NQ * PACK, BF16, AT_HI0)
-        lo0 = kept("lo0", NQ * PACK, BF16)
+        flipped = kept("flipped", NQ * PACK, BF16)
+        lo0 = laid("lo0", NQ * PACK, BF16, AT_LO0)
+        for m in range(TILES):
+            cols = slice(m * P * PACK, (m + 1) * P * PACK)
+            src = q_raw[0][:].rearrange("p (t m) -> p t m", t=PACK)[:, :, m * P : (m + 1) * P]
+            nc.scalar.activation(
+                flipped[:, cols].rearrange("p (c i t) -> p c t i", i=4, t=PACK),
+                src.rearrange("p t (c i) -> p c t i", i=4),
+                RELU,
+                scale=-1.0,
+            )
+            nc.vector.tensor_scalar_mul(lo0[:, cols], flipped[:, cols], -1.0)
+        quantise(C, 0, lo0, kept("codes_lo0", NQ, U32))
+        hi0 = kept("hi0", NQ * PACK, BF16)
         positive(0, hi0)
-        negative(0, lo0)
-        quantise(K, 0, hi0, kept("codes_hi0", NQ, U32))
 
-        first = gather(K, 0, AT_HI0)
-        middle = gather(K, 1, AT_HI0 + 512)
-        part_block(K, 0, first)
-        multiply(K, 0, 0)
-        part_block(K, 1, middle)
-        multiply(K, 0, 1)
-        last = gather(K, 2, AT_HI0)
-        quantise(C, 0, lo0, laid("codes_lo0", NQ, U32, AT_HI0 + 512))
-        part_block(K, 2, last)
-        multiply(K, 0, 2)
+        parted_k = [kept("parted_k0", PASSES * 384, U16), kept("parted_k1", PASSES * 128, U16)]
+        got_k = [gather(K, 0, 384, AT_LO0 + 512), gather(K, 384, 128, AT_LO0)]
+        quantise(K, 0, hi0, kept("codes_hi0", NQ, U32))
+        for parted, got in zip(parted_k, got_k):
+            nc.vector.tensor_copy(
+                parted[:].rearrange("p (o n) -> p o n", o=PASSES),
+                got[:].bitcast(U16).rearrange("p (n o) -> p o n", o=PASSES),
+            )
+        for o in range(PASSES):
+            words16[K, o, 0] = parted_k[0][:, o * 384 : o * 384 + 128]
+            words16[K, o, 1] = parted_k[0][:, o * 384 + 128 : (o + 1) * 384]
+            words16[K, o, 2] = parted_k[1][:, o * 128 : (o + 1) * 128]
+        for b in range(len(BLOCKS)):
+            multiply(K, 0, b)
 
         lo1 = laid("lo1", NQ * PACK, BF16, AT_K_WORDS)
         negative(1, lo1)
@@ -166,13 +198,13 @@ def tile_attend_quest_topk_kernel(tc, qT, k_words, k_scales, c_words, c_scales, 
         for b in range(len(BLOCKS)):
             multiply(K, 1, b)
 
-        first = gather(C, 0, AT_HI1)
-        middle = gather(C, 1, AT_HI1 + 1024)
+        first = gather(C, *BLOCKS[0], AT_HI1)
+        middle = gather(C, *BLOCKS[1], AT_HI1 + 1024)
         for b, got in ((0, first), (1, middle)):
             part_block(C, b, got)
             for o in range(PASSES):
                 multiply(C, o, b)
-        last = gather(C, 2, AT_HI1)
+        last = gather(C, *BLOCKS[2], AT_HI1)
         for o in range(PASSES):
             part_pass(C, 2, o, last)
             multiply(C, o, 2)

@@ -22,9 +22,11 @@ TILES = NQ // P
 K, C = 0, 1
 SCALE_ROW0 = (96, 32)
 SCALE_ZEROS = (((0, 96),), ((0, 32), (64, 128)))
+QUADS = (0, 2, 1, 3)
+WHOLE_QUAD = 1
 BLOCKS = ((0, 128), (128, 256), (384, 128))
 
-AT_LO0 = 0
+AT_FLIPPED = 0
 AT_HI1 = 8192
 AT_K_SCALES = 12288
 AT_K_WORDS = 20480
@@ -86,14 +88,17 @@ def tile_attend_quest_topk_kernel(tc, qT, k_words, k_scales, c_words, c_scales, 
         load_words(K, k_words, nc.scalar)
         load_q(1)
         got = gather_scales(K)
-        for quad in range(3):
-            move_pass(K, got, quad, 0)
-        move_both(K, got, 3)
+        for quad in QUADS:
+            if quad == WHOLE_QUAD:
+                move_both(K, got, quad)
+            else:
+                move_pass(K, got, quad, 0)
         load_words(C, c_words, nc.sync)
-        for quad in range(3):
-            move_pass(K, got, quad, 1)
+        for quad in QUADS:
+            if quad != WHOLE_QUAD:
+                move_pass(K, got, quad, 1)
         got = gather_scales(C)
-        for quad in range(4):
+        for quad in QUADS:
             move_both(C, got, quad)
 
         def interleaved(o, part):
@@ -157,8 +162,8 @@ def tile_attend_quest_topk_kernel(tc, qT, k_words, k_scales, c_words, c_scales, 
                     stop=(s == C and o == PASSES - 1),
                 )
 
-        flipped = kept("flipped", NQ * PACK, BF16)
-        lo0 = laid("lo0", NQ * PACK, BF16, AT_LO0)
+        flipped = laid("flipped", NQ * PACK, BF16, AT_FLIPPED)
+        lo0 = kept("lo0", NQ * PACK, BF16)
         for m in range(TILES):
             cols = slice(m * P * PACK, (m + 1) * P * PACK)
             src = q_raw[0][:].rearrange("p (t m) -> p t m", t=PACK)[:, :, m * P : (m + 1) * P]
@@ -174,7 +179,7 @@ def tile_attend_quest_topk_kernel(tc, qT, k_words, k_scales, c_words, c_scales, 
         positive(0, hi0)
 
         parted_k = [kept("parted_k0", PASSES * 384, U16), kept("parted_k1", PASSES * 128, U16)]
-        got_k = [gather(K, 0, 384, AT_LO0 + 512), gather(K, 384, 128, AT_LO0)]
+        got_k = [gather(K, 0, 384, AT_FLIPPED + 512), gather(K, 384, 128, AT_FLIPPED)]
         quantise(K, 0, hi0, kept("codes_hi0", NQ, U32))
         for parted, got in zip(parted_k, got_k):
             nc.vector.tensor_copy(

@@ -149,18 +149,21 @@ def tile_attend_quest_topk_kernel(tc, qT, k_words, k_scales, c_words, c_scales, 
             for b in range(len(BLOCKS))
         }
 
-        def multiply(s, o, b):
+        def multiply_tile(s, o, b, m):
             n0, width = BLOCKS[b]
+            nc.tensor.matmul_mx(
+                out=banks[m, b][:],
+                lhsT=q_codes[s, o][:, m * P : (m + 1) * P].bitcast(FP8X4),
+                lhsT_scale=q_scales[s, o][:, m * P : (m + 1) * P],
+                rhs=words16[s, o, b].bitcast(FP4X4),
+                rhs_scale=planes[s][:, o * N + n0 : o * N + n0 + width],
+                start=(s == K and o == 0),
+                stop=(s == C and o == PASSES - 1),
+            )
+
+        def multiply(s, o, b):
             for m in range(TILES):
-                nc.tensor.matmul_mx(
-                    out=banks[m, b][:],
-                    lhsT=q_codes[s, o][:, m * P : (m + 1) * P].bitcast(FP8X4),
-                    lhsT_scale=q_scales[s, o][:, m * P : (m + 1) * P],
-                    rhs=words16[s, o, b].bitcast(FP4X4),
-                    rhs_scale=planes[s][:, o * N + n0 : o * N + n0 + width],
-                    start=(s == K and o == 0),
-                    stop=(s == C and o == PASSES - 1),
-                )
+                multiply_tile(s, o, b, m)
 
         flipped = laid("flipped", NQ * PACK, BF16, AT_FLIPPED)
         lo0 = kept("lo0", NQ * PACK, BF16)
@@ -207,8 +210,9 @@ def tile_attend_quest_topk_kernel(tc, qT, k_words, k_scales, c_words, c_scales, 
         middle = gather(C, *BLOCKS[1], AT_HI1 + 1024)
         for b, got in ((0, first), (1, middle)):
             part_block(C, b, got)
-            for o in range(PASSES):
-                multiply(C, o, b)
+            for m in range(TILES):
+                for o in range(PASSES):
+                    multiply_tile(C, o, b, m)
         last = gather(C, *BLOCKS[2], AT_HI1)
         for o in range(PASSES):
             part_pass(C, 2, o, last)

@@ -24,7 +24,7 @@ SCALE_ROW0 = (96, 32)
 SCALE_ZEROS = (((0, 96),), ((0, 32), (64, 128)))
 QUADS = (0, 2, 1, 3)
 WHOLE_QUAD = 1
-BLOCKS = ((0, 128), (128, 256), (384, 128))
+BLOCKS = ((0, 128), (128, 128), (256, 128), (384, 128))
 
 AT_FLIPPED = 0
 AT_HI1 = 8192
@@ -133,15 +133,10 @@ def tile_attend_quest_topk_kernel(tc, qT, k_words, k_scales, c_words, c_scales, 
             parted = kept("parted%d_%d" % (s, b), PASSES * width, U16)
             nc.vector.tensor_copy(
                 parted[:].rearrange("p (o h n) -> p h o n", o=PASSES, h=2),
-                got[:].bitcast(U16).rearrange("p (h n o) -> p h o n", o=PASSES, h=2),
+                got.bitcast(U16).rearrange("p (h n o) -> p h o n", o=PASSES, h=2),
             )
             for o in range(PASSES):
                 words16[s, o, b] = parted[:, o * width : (o + 1) * width]
-
-        def part_pass(s, b, o, got):
-            parted = kept("parted%d_%d_%d" % (s, b, o), BLOCKS[b][1], U16)
-            nc.vector.tensor_copy(parted[:], got[:].bitcast(U16).rearrange("p (n o) -> p o n", o=PASSES)[:, o, :])
-            words16[s, o, b] = parted[:]
 
         banks = {
             (m, b): psum.tile([P, BLOCKS[b][1]], F32, name="bank%d_%d" % (m, b), tag="bank%d_%d" % (m, b))
@@ -190,9 +185,9 @@ def tile_attend_quest_topk_kernel(tc, qT, k_words, k_scales, c_words, c_scales, 
                 got[:].bitcast(U16).rearrange("p (n o) -> p o n", o=PASSES),
             )
         for o in range(PASSES):
-            words16[K, o, 0] = parted_k[0][:, o * 384 : o * 384 + 128]
-            words16[K, o, 1] = parted_k[0][:, o * 384 + 128 : (o + 1) * 384]
-            words16[K, o, 2] = parted_k[1][:, o * 128 : (o + 1) * 128]
+            for b in range(3):
+                words16[K, o, b] = parted_k[0][:, o * 384 + b * P : o * 384 + (b + 1) * P]
+            words16[K, o, 3] = parted_k[1][:, o * 128 : (o + 1) * 128]
         for b in range(len(BLOCKS)):
             multiply(K, 0, b)
 
@@ -206,17 +201,18 @@ def tile_attend_quest_topk_kernel(tc, qT, k_words, k_scales, c_words, c_scales, 
         for b in range(len(BLOCKS)):
             multiply(K, 1, b)
 
-        first = gather(C, *BLOCKS[0], AT_HI1)
-        middle = gather(C, *BLOCKS[1], AT_HI1 + 1024)
-        for b, got in ((0, first), (1, middle)):
-            part_block(C, b, got)
-            for m in range(TILES):
-                for o in range(PASSES):
-                    multiply_tile(C, o, b, m)
-        last = gather(C, *BLOCKS[2], AT_HI1)
-        for o in range(PASSES):
-            part_pass(C, 2, o, last)
-            multiply(C, o, 2)
+        ring = laid("got_c", 2 * P, U32, AT_HI1)
+        for pair in range(2):
+            for j in range(2):
+                n0 = BLOCKS[2 * pair + j][0]
+                lists = offsets[:, n0 // 16 : (n0 + P) // 16]
+                nc.vector.tensor_copy(ring[:, j * P : (j + 1) * P], word_win[C][:].bitcast(U32).indirect(lists))
+            for j in range(2):
+                b = 2 * pair + j
+                part_block(C, b, ring[:, j * P : (j + 1) * P])
+                for m in range(TILES):
+                    for o in range(PASSES):
+                        multiply_tile(C, o, b, m)
 
         out_by_tile = out[0].rearrange("(m p) n -> p m n", p=P)
 
@@ -234,6 +230,7 @@ def tile_attend_quest_topk_kernel(tc, qT, k_words, k_scales, c_words, c_scales, 
             nc.sync.dma_start(out_by_tile[:, :, n0 : n0 + width], staged[:].rearrange("p (m n) -> p m n", m=TILES))
 
         leave_both(0, (nc.scalar.copy, nc.scalar.copy))
-        leave_tile(1, 0, nc.scalar.copy)
-        leave_tile(1, 1, nc.vector.tensor_copy)
-        leave_both(2, (nc.vector.tensor_copy, nc.scalar.copy))
+        leave_both(1, (nc.scalar.copy, nc.scalar.copy))
+        leave_tile(2, 0, nc.vector.tensor_copy)
+        leave_tile(2, 1, nc.scalar.copy)
+        leave_both(3, (nc.vector.tensor_copy, nc.scalar.copy))

@@ -138,6 +138,11 @@ def tile_attend_quest_topk_kernel(tc, qT, k_words, k_scales, c_words, c_scales, 
             for o in range(PASSES):
                 words16[s, o, b] = parted[:, o * width : (o + 1) * width]
 
+        def part_pass(s, b, o, got):
+            parted = kept("parted%d_%d_%d" % (s, b, o), BLOCKS[b][1], U16)
+            nc.vector.tensor_copy(parted[:], got.bitcast(U16).rearrange("p (n o) -> p o n", o=PASSES)[:, o, :])
+            words16[s, o, b] = parted[:]
+
         banks = {
             (m, b): psum.tile([P, BLOCKS[b][1]], F32, name="bank%d_%d" % (m, b), tag="bank%d_%d" % (m, b))
             for m in range(TILES)
@@ -176,8 +181,8 @@ def tile_attend_quest_topk_kernel(tc, qT, k_words, k_scales, c_words, c_scales, 
         hi0 = kept("hi0", NQ * PACK, BF16)
         positive(0, hi0)
 
-        parted_k = [kept("parted_k0", PASSES * 384, U16), kept("parted_k1", PASSES * 128, U16)]
-        got_k = [gather(K, 0, 384, AT_FLIPPED + 512), gather(K, 384, 128, AT_FLIPPED)]
+        parted_k = [kept("parted_k%d" % h, N, U16) for h in range(2)]
+        got_k = [gather(K, h * 256, 256, AT_FLIPPED + h * 1024) for h in range(2)]
         quantise(K, 0, hi0, kept("codes_hi0", NQ, U32))
         for parted, got in zip(parted_k, got_k):
             nc.vector.tensor_copy(
@@ -185,9 +190,9 @@ def tile_attend_quest_topk_kernel(tc, qT, k_words, k_scales, c_words, c_scales, 
                 got[:].bitcast(U16).rearrange("p (n o) -> p o n", o=PASSES),
             )
         for o in range(PASSES):
-            for b in range(3):
-                words16[K, o, b] = parted_k[0][:, o * 384 + b * P : o * 384 + (b + 1) * P]
-            words16[K, o, 3] = parted_k[1][:, o * 128 : (o + 1) * 128]
+            for b in range(len(BLOCKS)):
+                c0 = o * 256 + (b % 2) * P
+                words16[K, o, b] = parted_k[b // 2][:, c0 : c0 + P]
         for b in range(len(BLOCKS)):
             multiply(K, 0, b)
 
@@ -209,10 +214,16 @@ def tile_attend_quest_topk_kernel(tc, qT, k_words, k_scales, c_words, c_scales, 
                 nc.vector.tensor_copy(ring[:, j * P : (j + 1) * P], word_win[C][:].bitcast(U32).indirect(lists))
             for j in range(2):
                 b = 2 * pair + j
-                part_block(C, b, ring[:, j * P : (j + 1) * P])
-                for m in range(TILES):
+                got = ring[:, j * P : (j + 1) * P]
+                if b == 3:
                     for o in range(PASSES):
-                        multiply_tile(C, o, b, m)
+                        part_pass(C, b, o, got)
+                        multiply(C, o, b)
+                else:
+                    part_block(C, b, got)
+                    for m in range(TILES):
+                        for o in range(PASSES):
+                            multiply_tile(C, o, b, m)
 
         out_by_tile = out[0].rearrange("(m p) n -> p m n", p=P)
 

from contextlib import ExitStack

import concourse.mybir as mybir

D, T, N, NQ = 1024, 2048, 512, 256
FLOPS = 2 * 2 * D * N * NQ

F32 = mybir.dt.float32
BF16 = mybir.dt.bfloat16
I32 = mybir.dt.int32
U32 = mybir.dt.uint32
U16 = mybir.dt.uint16
U8 = mybir.dt.uint8
FP8X4 = mybir.dt.float8_e4m3fn_x4
FP4X4 = mybir.dt.float4_e2m1fn_x4
RELU = mybir.ActivationFunctionType.Relu

P = 128
PACK = 4
PASSES = 2
TILES = NQ // P
K, C = 0, 1
SCALE_ROW0 = (96, 32)
SCALE_ZEROS = (((0, 96),), ((0, 32), (64, 128)))
QUADS = (0, 2, 1, 3)
WHOLE_QUAD = 1
BLOCKS = ((0, 128), (128, 128), (256, 128), (384, 128))

AT_FLIPPED = 0
AT_HI1 = 8192
AT_K_SCALES = 12288
AT_K_WORDS = 20480


def tile_attend_quest_topk_kernel(tc, qT, k_words, k_scales, c_words, c_scales, offs, out):
    nc = tc.nc
    with ExitStack() as ctx:
        keep = ctx.enter_context(tc.tile_pool(name="keep", bufs=1))
        reuse = ctx.enter_context(tc.tile_pool(name="reuse", bufs=1))
        psum = ctx.enter_context(tc.psum_pool(name="psum", bufs=1))

        def kept(name, width, dtype):
            return keep.tile([P, width], dtype, name=name, tag=name, align_bytes=64)

        def laid(name, width, dtype, offset):
            return reuse.tile([P, width], dtype, name=name, offset=offset, align_bytes=64)

        offsets = keep.tile([P, N // 16], U16, name="offsets")
        nc.sync.dma_start(offsets[:], offs)

        scale_win = [laid("k_scale_win", T, U8, AT_K_SCALES), kept("c_scale_win", T, U8)]
        for s, scales, queue in ((K, k_scales, nc.scalar), (C, c_scales, nc.sync)):
            row0 = SCALE_ROW0[s]
            queue.dma_start(scale_win[s][row0 : row0 + 32, :].bitcast(I32), scales.bitcast(I32).rearrange("o f w -> f o w"))
            for lo, hi in SCALE_ZEROS[s]:
                nc.vector.memset(scale_win[s][lo:hi, :].bitcast(I32), 0)
        planes = [kept("planes%d" % s, PASSES * N, U8) for s in (K, C)]
        for s in (K, C):
            nc.vector.memset(planes[s][:].bitcast(I32), 0)

        q_raw = [kept("q_raw%d" % o, PACK * NQ, F32) for o in range(PASSES)]
        word_win = [laid("k_word_win", T, I32, AT_K_WORDS), laid("c_word_win", T, I32, AT_K_SCALES)]

        def load_q(o):
            nc.scalar.dma_start(q_raw[o][:], qT[0, 512 * o : 512 * (o + 1), :].rearrange("(p t) m -> p (t m)", t=PACK))

        def load_words(s, words, queue):
            queue.dma_start(word_win[s][:], words[0].rearrange("p t b -> p (t b)").bitcast(I32))

        def gather_scales(s):
            got = kept("got_scales%d" % s, N, U8)
            nc.vector.tensor_copy(got[:], scale_win[s][:].indirect(offsets[:]))
            return got

        def move_both(s, got, quad):
            nc.sync.dma_start(
                planes[s][32 * quad : 32 * quad + 4, :].bitcast(I32).rearrange("p (o w) -> p o w", o=PASSES),
                got[SCALE_ROW0[s] + 8 * quad : SCALE_ROW0[s] + 8 * quad + 8, :].bitcast(I32),
            )

        def move_pass(s, got, quad, o):
            nc.sync.dma_start(
                planes[s][32 * quad : 32 * quad + 4, o * N : (o + 1) * N].bitcast(I32),
                got[SCALE_ROW0[s] + 8 * quad + o : SCALE_ROW0[s] + 8 * quad + 8 : 2, :].bitcast(I32),
            )

        load_q(0)
        load_words(K, k_words, nc.scalar)
        load_q(1)
        got = gather_scales(K)
        for quad in QUADS:
            if quad == WHOLE_QUAD:
                move_both(K, got, quad)
            else:
                move_pass(K, got, quad, 0)
        load_words(C, c_words, nc.sync)
        for quad in QUADS:
            if quad != WHOLE_QUAD:
                move_pass(K, got, quad, 1)
        got = gather_scales(C)
        for quad in QUADS:
            move_both(C, got, quad)

        def interleaved(o, part):
            src = q_raw[o][:].rearrange("p (t c i) -> p c t i", t=PACK, i=4)
            return part[:].rearrange("p (c i t) -> p c t i", i=4, t=PACK), src

        def positive(o, part):
            dst, src = interleaved(o, part)
            nc.scalar.activation(dst, src, RELU)

        def negative(o, part):
            dst, src = interleaved(o, part)
            nc.vector.tensor_scalar_min(dst, src, 0.0)

        q_codes, q_scales = {}, {}

        def quantise(s, o, part, codes):
            scales = kept("q_scales%d_%d" % (s, o), NQ, U8)
            nc.vector.quantize_mx(out=codes[:].bitcast(FP8X4), scales=scales[:], in_=part[:])
            q_codes[s, o], q_scales[s, o] = codes, scales

        def gather(s, n0, width, at):
            got = laid("got%d_%d" % (s, n0), width, U32, at)
            lists = offsets[:, n0 // 16 : (n0 + width) // 16]
            nc.vector.tensor_copy(got[:], word_win[s][:].bitcast(U32).indirect(lists))
            return got

        words16 = {}

        def part_block(s, b, got):
            width = BLOCKS[b][1]
            parted = kept("parted%d_%d" % (s, b), PASSES * width, U16)
            nc.vector.tensor_copy(
                parted[:].rearrange("p (o h n) -> p h o n", o=PASSES, h=2),
                got.bitcast(U16).rearrange("p (h n o) -> p h o n", o=PASSES, h=2),
            )
            for o in range(PASSES):
                words16[s, o, b] = parted[:, o * width : (o + 1) * width]

        def part_pass(s, b, o, got):
            parted = kept("parted%d_%d_%d" % (s, b, o), BLOCKS[b][1], U16)
            nc.vector.tensor_copy(parted[:], got.bitcast(U16).rearrange("p (n o) -> p o n", o=PASSES)[:, o, :])
            words16[s, o, b] = parted[:]

        banks = {
            (m, b): psum.tile([P, BLOCKS[b][1]], F32, name="bank%d_%d" % (m, b), tag="bank%d_%d" % (m, b))
            for m in range(TILES)
            for b in range(len(BLOCKS))
        }

        def multiply_tile(s, o, b, m):
            n0, width = BLOCKS[b]
            nc.tensor.matmul_mx(
                out=banks[m, b][:],
                lhsT=q_codes[s, o][:, m * P : (m + 1) * P].bitcast(FP8X4),
                lhsT_scale=q_scales[s, o][:, m * P : (m + 1) * P],
                rhs=words16[s, o, b].bitcast(FP4X4),
                rhs_scale=planes[s][:, o * N + n0 : o * N + n0 + width],
                start=(s == K and o == 0),
                stop=(s == C and o == PASSES - 1),
            )

        def multiply(s, o, b):
            for m in range(TILES):
                multiply_tile(s, o, b, m)

        flipped = laid("flipped", NQ * PACK, BF16, AT_FLIPPED)
        lo0 = kept("lo0", NQ * PACK, BF16)
        for m in range(TILES):
            cols = slice(m * P * PACK, (m + 1) * P * PACK)
            src = q_raw[0][:].rearrange("p (t m) -> p t m", t=PACK)[:, :, m * P : (m + 1) * P]
            nc.scalar.activation(
                flipped[:, cols].rearrange("p (c i t) -> p c t i", i=4, t=PACK),
                src.rearrange("p t (c i) -> p c t i", i=4),
                RELU,
                scale=-1.0,
            )
            nc.vector.tensor_scalar_mul(lo0[:, cols], flipped[:, cols], -1.0)
        quantise(C, 0, lo0, kept("codes_lo0", NQ, U32))
        hi0 = kept("hi0", NQ * PACK, BF16)
        positive(0, hi0)

        parted_k = [kept("parted_k%d" % h, N, U16) for h in range(2)]
        got_k = [gather(K, h * 256, 256, AT_FLIPPED + h * 1024) for h in range(2)]
        quantise(K, 0, hi0, kept("codes_hi0", NQ, U32))
        for parted, got in zip(parted_k, got_k):
            nc.vector.tensor_copy(
                parted[:].rearrange("p (o n) -> p o n", o=PASSES),
                got[:].bitcast(U16).rearrange("p (n o) -> p o n", o=PASSES),
            )
        for o in range(PASSES):
            for b in range(len(BLOCKS)):
                c0 = o * 256 + (b % 2) * P
                words16[K, o, b] = parted_k[b // 2][:, c0 : c0 + P]
        for b in range(len(BLOCKS)):
            multiply(K, 0, b)

        lo1 = laid("lo1", NQ * PACK, BF16, AT_K_WORDS)
        negative(1, lo1)

        hi1 = laid("hi1", NQ * PACK, BF16, AT_HI1)
        positive(1, hi1)
        quantise(K, 1, hi1, laid("codes_hi1", NQ, U32, AT_K_WORDS + 2048))
        quantise(C, 1, lo1, kept("codes_lo1", NQ, U32))
        for b in range(len(BLOCKS)):
            multiply(K, 1, b)

        ring = laid("got_c", 2 * P, U32, AT_HI1)
        for pair in range(2):
            for j in range(2):
                n0 = BLOCKS[2 * pair + j][0]
                lists = offsets[:, n0 // 16 : (n0 + P) // 16]
                nc.vector.tensor_copy(ring[:, j * P : (j + 1) * P], word_win[C][:].bitcast(U32).indirect(lists))
            for j in range(2):
                b = 2 * pair + j
                got = ring[:, j * P : (j + 1) * P]
                if b == 3:
                    for o in range(PASSES):
                        part_pass(C, b, o, got)
                        multiply(C, o, b)
                else:
                    part_block(C, b, got)
                    for m in range(TILES):
                        for o in range(PASSES):
                            multiply_tile(C, o, b, m)

        out_by_tile = out[0].rearrange("(m p) n -> p m n", p=P)

        def leave_tile(b, m, copy):
            n0, width = BLOCKS[b]
            staged = kept("staged%d_%d" % (b, m), width, F32)
            copy(staged[:], banks[m, b][:])
            nc.sync.dma_start(out[0, m * P : (m + 1) * P, n0 : n0 + width], staged[:])

        def leave_both(b, copies):
            n0, width = BLOCKS[b]
            staged = kept("staged%d" % b, TILES * width, F32)
            for m in range(TILES):
                copies[m](staged[:, m * width : (m + 1) * width], banks[m, b][:])
            nc.sync.dma_start(out_by_tile[:, :, n0 : n0 + width], staged[:].rearrange("p (m n) -> p m n", m=TILES))

        leave_both(0, (nc.scalar.copy, nc.scalar.copy))
        leave_both(1, (nc.scalar.copy, nc.scalar.copy))
        leave_tile(2, 0, nc.vector.tensor_copy)
        leave_tile(2, 1, nc.scalar.copy)
        leave_both(3, (nc.vector.tensor_copy, nc.scalar.copy))
